import numpy as np
import ml_dtypes


def mxq(x, axis, fmt="e4m3"):
    dtype, down = {"e4m3": (ml_dtypes.float8_e4m3fn, 7), "e5m2": (ml_dtypes.float8_e5m2, 14)}[fmt]
    v = np.moveaxis(np.asarray(x, np.float32).astype(ml_dtypes.bfloat16).astype(np.float64), axis, -1)
    blocks = v.reshape(v.shape[:-1] + (-1, 32))
    amax = np.abs(blocks).max(-1, keepdims=True)
    byte = np.maximum(np.where(amax > 0, np.frexp(amax)[1] - 1 + 127, 0) - down, 1)
    scale = np.exp2(byte - 127.0)
    codes = (blocks / scale).astype(np.float32).astype(dtype).astype(np.float64)
    return np.moveaxis((codes * scale).reshape(v.shape), -1, axis)


WIDE = False


def mx_kscale(k):
    if not WIDE:
        return np.ones(k)
    levels = np.array([10, -10, 5, -5, 0])
    if k % 512:
        return np.exp2(np.random.permutation(np.resize(levels, k // 32))).repeat(32)
    a = np.empty((k // 512, 16))
    for p in range(k // 512):
        a[p, :8] = np.random.permutation(np.resize(levels, 8))
        for g in range(8):
            far = levels[np.abs(levels - a[p, g]) >= 10]
            a[p, g + 8] = far[np.random.randint(len(far))]
    return np.exp2(a.ravel()).repeat(32)


def f64(x):
    return np.asarray(x).astype(np.float64)


def striped(idx):
    return np.tile(idx.reshape(-1, 16).T, (8, 1)).astype(np.uint16)


def unstriped(offs):
    return offs[:16].T.reshape(-1).astype(np.int64)


def pack_weight(w):
    k, n = w.shape
    w = f64(np.asarray(w, np.float32).astype(ml_dtypes.bfloat16)).reshape(k // 32, 32, n)
    amax = np.abs(w).max(1)
    byte = np.clip(np.where(amax > 0, np.frexp(amax)[1] - 1 + 127 - 7, 1), 1, 254)
    scaled = (w * np.exp2(127.0 - byte)[:, None, :]).reshape(k, n).astype(np.float32)
    words = np.ascontiguousarray(scaled.reshape(k // 512, 128, 4, n).transpose(0, 1, 3, 2)).astype(ml_dtypes.float8_e4m3fn).view(np.uint8)
    return words, np.ascontiguousarray(byte.astype(np.uint8).reshape(k // 512, 16, n))


def unpack_weight(words, scales):
    g, p, n, _ = words.shape
    vals = np.ascontiguousarray(words).view(ml_dtypes.float8_e4m3fn).astype(np.float64) * np.repeat(np.exp2(scales.astype(np.float64) - 127.0), 8, axis=1)[..., None]
    return vals.transpose(0, 1, 3, 2).reshape(g * 512, n)


def gelu(v):
    return 0.5 * v * (1.0 + np.tanh(np.sqrt(2.0 / np.pi) * (v + 0.044715 * v**3)))


K, T, S, V, N = 512, 4096, 1024, 512, 256


def setup_inputs():
    n = np.random.standard_normal
    s = mx_kscale(K)[:, None]
    packed_xT = pack_weight(n((K, T)) * s)
    return {
        "x_words": packed_xT[0],
        "x_scales": packed_xT[1],
        "w1": (n((K, N)) / np.sqrt(K) / s).astype(np.float32),
        "offs": striped(np.random.permutation(T)[:S]),
        "pos1": striped(np.random.permutation(S)[:V]),
        "pos2": striped(np.random.permutation(S)[:V]),
        "pos3": striped(np.random.permutation(S)[:V]),
    }


def reference(x_words, x_scales, w1, offs, pos1, pos2, pos3):
    xq = unpack_weight(x_words, x_scales)[:, unstriped(offs)]
    y = gelu(mxq(f64(w1), 0, "e4m3").T @ xq)
    n0 = y[:, unstriped(pos1)]
    n1 = y[:, unstriped(pos2)]
    n2 = y[:, unstriped(pos3)]
    return np.maximum(np.minimum(n0, n1), np.minimum(np.maximum(n0, n1), n2))

@@ -1,0 +1,123 @@
+from contextlib import ExitStack
+
+import concourse.mybir as mybir
+
+K, T, S, V, N = 512, 4096, 1024, 512, 256
+FLOPS = 2 * K * N * S
+
+F32 = mybir.dt.float32
+BF16 = mybir.dt.bfloat16
+I32 = mybir.dt.int32
+U32 = mybir.dt.uint32
+U16 = mybir.dt.uint16
+U8 = mybir.dt.uint8
+FP8X4 = mybir.dt.float8_e4m3fn_x4
+GELU = mybir.ActivationFunctionType.Gelu_apprx_tanh
+MAX = mybir.AluOpType.max
+MIN = mybir.AluOpType.min
+
+P = 128
+PACK = 4
+LANES = 16
+CHUNK = 512
+
+
+def tile_picked_median_gelu_p_kernel(
+    tc, x_words, x_scales, w1, offs, pos1, pos2, pos3, out
+):
+    nc = tc.nc
+    with ExitStack() as ctx:
+        keep = ctx.enter_context(tc.tile_pool(name="keep", bufs=1))
+        psum = ctx.enter_context(tc.psum_pool(name="psum", bufs=1))
+
+        offs_t = keep.tile([P, S // LANES], U16, name="offs_t")
+        nc.sync.dma_start(offs_t[:], offs)
+
+        scale_table = keep.tile([P, T], U8, name="scale_table", tag="scale_table_then_words", align_bytes=64)
+        nc.vector.memset(scale_table[:].bitcast(I32), 0)
+        nc.scalar.dma_start(scale_table[0:P:8, :].bitcast(I32), x_scales[0].bitcast(I32))
+
+        w_rows = w1.rearrange("(p j) m -> p j m", j=PACK)
+        w_raw = [keep.tile([P, PACK, P], F32, name="w_raw0")]
+        nc.sync.dma_start(w_raw[0][:], w_rows[:, :, 0:P])
+        word_table = keep.tile([P, T], I32, name="word_table", align_bytes=64)
+        nc.sync.dma_start(word_table[:], x_words[0].rearrange("p n t -> p (n t)").bitcast(I32))
+        pos_t = []
+        for i, pos in enumerate((pos1, pos2, pos3)):
+            t = keep.tile([P, V // LANES], U16, name=f"pos_t{i}")
+            nc.sync.dma_start(t[:], pos)
+            pos_t.append(t)
+
+        picked_scales = keep.tile([P, S], U8, name="picked_scales", tag="scales_then_w", align_bytes=64)
+        nc.vector.tensor_copy(picked_scales[:], scale_table[:].indirect(offs_t[:]))
+        x_plane = keep.tile([P, S], U8, name="x_plane", align_bytes=64)
+        nc.vector.tensor_copy(x_plane[:].bitcast(I32), picked_scales[:].bitcast(I32))
+        for r in range(1, 4):
+            nc.scalar.dma_start(x_plane[r:P:32, :].bitcast(I32), picked_scales[8 * r : P : 32, :].bitcast(I32))
+        w_raw.append(keep.tile([P, PACK, P], F32, name="w_raw1", tag="scales_then_w", align_bytes=64))
+        nc.sync.dma_start(w_raw[1][:], w_rows[:, :, P : 2 * P])
+
+        def quantize_w(h):
+            grouped = keep.tile([P, P, PACK], BF16, name=f"w_grouped{h}", align_bytes=64)
+            nc.vector.tensor_copy(
+                grouped[:].rearrange("p (c i) j -> p c j i", i=4),
+                w_raw[h][:].rearrange("p j (c i) -> p c j i", i=4),
+            )
+            codes = keep.tile([P, P], U32, name=f"w_codes{h}", align_bytes=64)
+            plane = keep.tile([P, P], U8, name=f"w_plane{h}", align_bytes=64)
+            nc.vector.quantize_mx(
+                out=codes[:].bitcast(FP8X4), scales=plane[:], in_=grouped[:].rearrange("p c j -> p (c j)")
+            )
+            return codes, plane
+
+        w_q = [quantize_w(0)]
+
+        picked = []
+        for c in range(S // CHUNK):
+            t = keep.tile([P, CHUNK], U32, name=f"picked{c}", tag=("scale_table_then_words" if c == 0 else "picked1"), align_bytes=64)
+            cols = slice(c * CHUNK // LANES, (c + 1) * CHUNK // LANES)
+            nc.vector.tensor_copy(t[:], word_table[:].bitcast(U32).indirect(offs_t[:, cols]))
+            picked.append(t)
+
+        w_q.append(quantize_w(1))
+
+        pieces = [[(0, 512), (512, 128), (640, 128), (768, 128), (896, 128)], [(0, 512), (512, 512)]]
+        y = []
+        for h in range(2):
+            codes, plane = w_q[h]
+            y_h = keep.tile([P, S], F32, name=f"y{h}")
+            for s0, n in pieces[h]:
+                acc = psum.tile([P, n], F32, name=f"acc{h}_{s0}")
+                c, o = divmod(s0, CHUNK)
+                nc.tensor.matmul_mx(
+                    out=acc[:],
+                    lhsT=codes[:].bitcast(FP8X4),
+                    lhsT_scale=plane[:],
+                    rhs=picked[c][:, o : o + n].bitcast(FP8X4),
+                    rhs_scale=x_plane[:, s0 : s0 + n],
+                    start=True,
+                    stop=True,
+                )
+                nc.scalar.activation(y_h[:, s0 : s0 + n], acc[:], GELU)
+            y.append(y_h)
+
+        cuts = [[(0, 256), (256, 256)], [(0, 256), (256, 128), (384, 128)]]
+        for h in range(2):
+            nb = []
+            for i in range(3):
+                t = keep.tile([P, V], F32, name=f"nb{h}_{i}")
+                nc.vector.tensor_copy(t[:], y[h][:].indirect(pos_t[i][:]))
+                nb.append(t)
+            hi = keep.tile([P, V], F32, name=f"hi{h}")
+            lo = keep.tile([P, V], F32, name=f"lo{h}")
+            nc.vector.tensor_tensor(hi[:], nb[0][:], nb[1][:], MAX)
+            nc.vector.tensor_tensor(lo[:], nb[0][:], nb[1][:], MIN)
+            capped = []
+            for v0, n in cuts[h]:
+                t = keep.tile([P, n], F32, name=f"cap{h}_{v0}")
+                nc.vector.tensor_tensor(t[:], hi[:, v0 : v0 + n], nb[2][:, v0 : v0 + n], MIN)
+                capped.append(t)
+            for j, (v0, n) in enumerate(cuts[h]):
+                t = keep.tile([P, n], F32, name=f"med{h}_{v0}")
+                nc.vector.tensor_tensor(t[:], capped[j][:], lo[:, v0 : v0 + n], MAX)
+                nc.sync.dma_start(out[h * P : (h + 1) * P, v0 : v0 + n], t[:])

@@ -31,31 +31,30 @@ def tile_picked_median_gelu_p_kernel(
         psum = ctx.enter_context(tc.psum_pool(name="psum", bufs=1))
 
         offs_t = keep.tile([P, S // LANES], U16, name="offs_t")
-        nc.sync.dma_start(offs_t[:], offs)
-
+        pos_t = [keep.tile([P, V // LANES], U16, name=f"pos_t{i}") for i in range(3)]
         scale_table = keep.tile([P, T], U8, name="scale_table", tag="scale_table_then_words", align_bytes=64)
-        nc.vector.memset(scale_table[:].bitcast(I32), 0)
-        nc.scalar.dma_start(scale_table[0:P:8, :].bitcast(I32), x_scales[0].bitcast(I32))
-
         w_rows = w1.rearrange("(p j) m -> p j m", j=PACK)
-        w_raw = [keep.tile([P, PACK, P], F32, name="w_raw0")]
-        nc.sync.dma_start(w_raw[0][:], w_rows[:, :, 0:P])
+        w_raw = [keep.tile([P, PACK, P], F32, name=f"w_raw{h}") for h in range(2)]
         word_table = keep.tile([P, T], I32, name="word_table", align_bytes=64)
+        nc.sync.dma_start(scale_table[112:P, :].bitcast(I32), x_scales[0].bitcast(I32))
+        nc.sync.dma_start(offs_t[:], offs)
+        nc.sync.dma_start(w_raw[0][:], w_rows[:, :, 0 * P : 1 * P])
+        nc.sync.dma_start(pos_t[0][:], pos1)
         nc.sync.dma_start(word_table[:], x_words[0].rearrange("p n t -> p (n t)").bitcast(I32))
-        pos_t = []
-        for i, pos in enumerate((pos1, pos2, pos3)):
-            t = keep.tile([P, V // LANES], U16, name=f"pos_t{i}")
-            nc.sync.dma_start(t[:], pos)
-            pos_t.append(t)
+        nc.sync.dma_start(w_raw[1][:], w_rows[:, :, 1 * P : 2 * P])
+        nc.sync.dma_start(pos_t[1][:], pos2)
+        nc.sync.dma_start(pos_t[2][:], pos3)
+        nc.vector.memset(scale_table[0:112, :].bitcast(I32), 0)
 
-        picked_scales = keep.tile([P, S], U8, name="picked_scales", tag="scales_then_w", align_bytes=64)
+        picked_scales = keep.tile([P, S], U8, name="picked_scales", align_bytes=64)
         nc.vector.tensor_copy(picked_scales[:], scale_table[:].indirect(offs_t[:]))
         x_plane = keep.tile([P, S], U8, name="x_plane", align_bytes=64)
-        nc.vector.tensor_copy(x_plane[:].bitcast(I32), picked_scales[:].bitcast(I32))
-        for r in range(1, 4):
-            nc.scalar.dma_start(x_plane[r:P:32, :].bitcast(I32), picked_scales[8 * r : P : 32, :].bitcast(I32))
-        w_raw.append(keep.tile([P, PACK, P], F32, name="w_raw1", tag="scales_then_w", align_bytes=64))
-        nc.sync.dma_start(w_raw[1][:], w_rows[:, :, P : 2 * P])
+        nc.vector.memset(x_plane[:].bitcast(I32), 0)
+        for q in range(4):
+            nc.scalar.dma_start(
+                x_plane[32 * q : 32 * q + 4, :].bitcast(I32), picked_scales[112 + 4 * q : 116 + 4 * q, :].bitcast(I32)
+            )
+
 
         def quantize_w(h):
             grouped = keep.tile([P, P, PACK], BF16, name=f"w_grouped{h}", align_bytes=64)
@@ -72,12 +71,12 @@ def tile_picked_median_gelu_p_kernel(
 
         w_q = [quantize_w(0)]
 
-        picked = []
+        picked = keep.tile([P, S], U32, name="picked", tag="scale_table_then_words", align_bytes=64)
         for c in range(S // CHUNK):
-            t = keep.tile([P, CHUNK], U32, name=f"picked{c}", tag=("scale_table_then_words" if c == 0 else "picked1"), align_bytes=64)
             cols = slice(c * CHUNK // LANES, (c + 1) * CHUNK // LANES)
-            nc.vector.tensor_copy(t[:], word_table[:].bitcast(U32).indirect(offs_t[:, cols]))
-            picked.append(t)
+            nc.vector.tensor_copy(
+                picked[:, c * CHUNK : (c + 1) * CHUNK], word_table[:].bitcast(U32).indirect(offs_t[:, cols])
+            )
 
         w_q.append(quantize_w(1))
 
@@ -88,12 +87,11 @@ def tile_picked_median_gelu_p_kernel(
             y_h = keep.tile([P, S], F32, name=f"y{h}")
             for s0, n in pieces[h]:
                 acc = psum.tile([P, n], F32, name=f"acc{h}_{s0}")
-                c, o = divmod(s0, CHUNK)
                 nc.tensor.matmul_mx(
                     out=acc[:],
                     lhsT=codes[:].bitcast(FP8X4),
                     lhsT_scale=plane[:],
-                    rhs=picked[c][:, o : o + n].bitcast(FP8X4),
+                    rhs=picked[:, s0 : s0 + n].bitcast(FP8X4),
                     rhs_scale=x_plane[:, s0 : s0 + n],
                     start=True,
                     stop=True,
@@ -120,4 +118,4 @@ def tile_picked_median_gelu_p_kernel(
             for j, (v0, n) in enumerate(cuts[h]):
                 t = keep.tile([P, n], F32, name=f"med{h}_{v0}")
                 nc.vector.tensor_tensor(t[:], capped[j][:], lo[:, v0 : v0 + n], MAX)
-                nc.sync.dma_start(out[h * P : (h + 1) * P, v0 : v0 + n], t[:])
+                (nc.scalar if j % 2 else nc.sync).dma_start(out[h * P : (h + 1) * P, v0 : v0 + n], t[:])

@@ -1,6 +1,7 @@
 from contextlib import ExitStack
 
 import concourse.mybir as mybir
+from concourse.masks import make_identity
 
 K, T, S, V, N = 512, 4096, 1024, 512, 256
 FLOPS = 2 * K * N * S
@@ -15,6 +16,10 @@ FP8X4 = mybir.dt.float8_e4m3fn_x4
 GELU = mybir.ActivationFunctionType.Gelu_apprx_tanh
 MAX = mybir.AluOpType.max
 MIN = mybir.AluOpType.min
+ADD = mybir.AluOpType.add
+SUB = mybir.AluOpType.subtract
+COPY = mybir.ActivationFunctionType.Copy
+ABS = mybir.ActivationFunctionType.Abs
 
 P = 128
 PACK = 4
@@ -80,13 +85,18 @@ def tile_picked_median_gelu_p_kernel(
 
         w_q.append(quantize_w(1))
 
+        ident = keep.tile([P, P], F32, name="ident")
+        make_identity(nc, ident[:])
+
         pieces = [[(0, 512), (512, 128), (640, 128), (768, 128), (896, 128)], [(0, 512), (512, 512)]]
         y = []
+        bank = 0
         for h in range(2):
             codes, plane = w_q[h]
             y_h = keep.tile([P, S], F32, name=f"y{h}")
             for s0, n in pieces[h]:
-                acc = psum.tile([P, n], F32, name=f"acc{h}_{s0}")
+                acc = psum.tile([P, n], F32, name=f"acc{h}_{s0}", tag=f"bank{bank}")
+                bank = bank + 1
                 nc.tensor.matmul_mx(
                     out=acc[:],
                     lhsT=codes[:].bitcast(FP8X4),
@@ -99,23 +109,77 @@ def tile_picked_median_gelu_p_kernel(
                 nc.scalar.activation(y_h[:, s0 : s0 + n], acc[:], GELU)
             y.append(y_h)
 
-        cuts = [[(0, 256), (256, 256)], [(0, 256), (256, 128), (384, 128)]]
-        for h in range(2):
-            nb = []
-            for i in range(3):
-                t = keep.tile([P, V], F32, name=f"nb{h}_{i}")
-                nc.vector.tensor_copy(t[:], y[h][:].indirect(pos_t[i][:]))
-                nb.append(t)
-            hi = keep.tile([P, V], F32, name=f"hi{h}")
-            lo = keep.tile([P, V], F32, name=f"lo{h}")
-            nc.vector.tensor_tensor(hi[:], nb[0][:], nb[1][:], MAX)
-            nc.vector.tensor_tensor(lo[:], nb[0][:], nb[1][:], MIN)
-            capped = []
-            for v0, n in cuts[h]:
-                t = keep.tile([P, n], F32, name=f"cap{h}_{v0}")
-                nc.vector.tensor_tensor(t[:], hi[:, v0 : v0 + n], nb[2][:, v0 : v0 + n], MIN)
-                capped.append(t)
-            for j, (v0, n) in enumerate(cuts[h]):
-                t = keep.tile([P, n], F32, name=f"med{h}_{v0}")
-                nc.vector.tensor_tensor(t[:], capped[j][:], lo[:, v0 : v0 + n], MAX)
-                (nc.scalar if j % 2 else nc.sync).dma_start(out[h * P : (h + 1) * P, v0 : v0 + n], t[:])
+        W = 256
+        parts = [(0, 0), (0, W), (1, 0), (1, W)]
+        ab, lo, spread, rise = {}, {}, {}, {}
+
+        def nbr(k, i):
+            h, v0 = parts[k]
+            return y[h][:].indirect(pos_t[i][:, v0 // LANES : (v0 + W) // LANES])
+
+        def fetch(k, i):
+            if i == 0:
+                ab[k] = keep.tile([P, 2, W], F32, name=f"ab{k}", tag=f"hold{k - 2}")
+            nc.vector.tensor_copy(ab[k][:, i, :], nbr(k, i))
+
+        diff_banks = [(0, 1), (3, 4), (5, 6), (1, 3)]
+        spread_banks = [2, 7, 0, 4]
+
+        def make_spread(k):
+            neg = keep.tile([P, W], F32, name=f"neg{k}")
+            nc.scalar.activation(neg[:], ab[k][:, 0, :], COPY, scale=-1.0)
+            blocks = [slice(j * P, (j + 1) * P) for j in range(W // P)]
+            diff = [psum.tile([P, P], F32, name=f"diff{k}_{j}", tag=f"bank{diff_banks[k][j]}") for j in range(W // P)]
+            for j, c in enumerate(blocks):
+                nc.tensor.matmul(diff[j][:], neg[:, c], ident[:], is_transpose=True, start=True, stop=False)
+            for j, c in enumerate(blocks):
+                nc.tensor.matmul(diff[j][:], ab[k][:, 1, c], ident[:], is_transpose=True, start=False, stop=True)
+            turned = keep.tile([P, W], F32, name=f"turned{k}", tag=f"hold{k}")
+            spread[k] = psum.tile([P, W], F32, name=f"spread{k}", tag=f"bank{spread_banks[k]}")
+            for j, c in enumerate(blocks):
+                nc.scalar.activation(turned[:, c], diff[j][:], ABS)
+            for j, c in enumerate(blocks):
+                nc.tensor.transpose(spread[k][:, c], turned[:, c], ident[:])
+
+        def make_lo(k):
+            lo[k] = keep.tile([P, W], F32, name=f"lo{k}", tag="rise1" if k == 2 else f"lo{k}")
+            nc.vector.tensor_tensor(lo[k][:], ab[k][:, 0, :], ab[k][:, 1, :], MIN)
+
+        def make_rise(k):
+            rise[k] = keep.tile([P, W], F32, name=f"rise{k}")
+            nc.vector.tensor_tensor(rise[k][:], nbr(k, 2), lo[k][:], SUB)
+
+        step = {}
+
+        def make_step(k):
+            step[k] = keep.tile([P, W], F32, name=f"step{k}")
+            nc.vector.scalar_tensor_tensor(step[k][:], rise[k][:], 0.0, spread[k][:], MAX, MIN)
+
+        def finish(k, engine, queue):
+            h, v0 = parts[k]
+            med = keep.tile([P, W], F32, name=f"med{k}")
+            engine.tensor_tensor(med[:], lo[k][:], step[k][:], ADD)
+            queue.dma_start(out[h * P : (h + 1) * P, v0 : v0 + W], med[:])
+
+        for k in (0, 1):
+            fetch(k, 0)
+            fetch(k, 1)
+            make_spread(k)
+        for k in (0, 1):
+            make_lo(k)
+        for k in (0, 1):
+            make_rise(k)
+        for k in (0, 1):
+            make_step(k)
+            finish(k, nc.gpsimd, nc.sync)
+            fetch(k + 2, 0)
+            fetch(k + 2, 1)
+            make_spread(k + 2)
+        for k in (2, 3):
+            make_lo(k)
+        for k in (2, 3):
+            make_rise(k)
+        for k in (2, 3):
+            make_step(k)
+        finish(2, nc.vector, nc.sync)
+        finish(3, nc.vector, nc.scalar)

@@ -14,17 +14,20 @@ U16 = mybir.dt.uint16
 U8 = mybir.dt.uint8
 FP8X4 = mybir.dt.float8_e4m3fn_x4
 GELU = mybir.ActivationFunctionType.Gelu_apprx_tanh
+COPY = mybir.ActivationFunctionType.Copy
+ABS = mybir.ActivationFunctionType.Abs
 MAX = mybir.AluOpType.max
 MIN = mybir.AluOpType.min
 ADD = mybir.AluOpType.add
 SUB = mybir.AluOpType.subtract
-COPY = mybir.ActivationFunctionType.Copy
-ABS = mybir.ActivationFunctionType.Abs
 
 P = 128
 PACK = 4
 LANES = 16
+BLOCKS = K // 32
+ROW0 = P - BLOCKS
 CHUNK = 512
+PART = 256
 
 
 def tile_picked_median_gelu_p_kernel(
@@ -41,7 +44,7 @@ def tile_picked_median_gelu_p_kernel(
         w_rows = w1.rearrange("(p j) m -> p j m", j=PACK)
         w_raw = [keep.tile([P, PACK, P], F32, name=f"w_raw{h}") for h in range(2)]
         word_table = keep.tile([P, T], I32, name="word_table", align_bytes=64)
-        nc.sync.dma_start(scale_table[112:P, :].bitcast(I32), x_scales[0].bitcast(I32))
+        nc.sync.dma_start(scale_table[ROW0:P, :].bitcast(I32), x_scales[0].bitcast(I32))
         nc.sync.dma_start(offs_t[:], offs)
         nc.sync.dma_start(w_raw[0][:], w_rows[:, :, 0 * P : 1 * P])
         nc.sync.dma_start(pos_t[0][:], pos1)
@@ -49,7 +52,7 @@ def tile_picked_median_gelu_p_kernel(
         nc.sync.dma_start(w_raw[1][:], w_rows[:, :, 1 * P : 2 * P])
         nc.sync.dma_start(pos_t[1][:], pos2)
         nc.sync.dma_start(pos_t[2][:], pos3)
-        nc.vector.memset(scale_table[0:112, :].bitcast(I32), 0)
+        nc.vector.memset(scale_table[0:ROW0, :].bitcast(I32), 0)
 
         picked_scales = keep.tile([P, S], U8, name="picked_scales", align_bytes=64)
         nc.vector.tensor_copy(picked_scales[:], scale_table[:].indirect(offs_t[:]))
@@ -57,9 +60,9 @@ def tile_picked_median_gelu_p_kernel(
         nc.vector.memset(x_plane[:].bitcast(I32), 0)
         for q in range(4):
             nc.scalar.dma_start(
-                x_plane[32 * q : 32 * q + 4, :].bitcast(I32), picked_scales[112 + 4 * q : 116 + 4 * q, :].bitcast(I32)
+                x_plane[32 * q : 32 * q + 4, :].bitcast(I32),
+                picked_scales[ROW0 + 4 * q : ROW0 + 4 * q + 4, :].bitcast(I32),
             )
-
 
         def quantize_w(h):
             grouped = keep.tile([P, P, PACK], BF16, name=f"w_grouped{h}", align_bytes=64)
@@ -85,10 +88,10 @@ def tile_picked_median_gelu_p_kernel(
 
         w_q.append(quantize_w(1))
 
-        ident = keep.tile([P, P], F32, name="ident")
+        ident = keep.tile([P, P], F32, name="ident", tag="w_grouped0", align_bytes=64)
         make_identity(nc, ident[:])
 
-        pieces = [[(0, 512), (512, 128), (640, 128), (768, 128), (896, 128)], [(0, 512), (512, 512)]]
+        pieces = [[(0, CHUNK)] + [(s0, P) for s0 in range(CHUNK, S, P)], [(0, CHUNK), (CHUNK, CHUNK)]]
         y = []
         bank = 0
         for h in range(2):
@@ -109,77 +112,78 @@ def tile_picked_median_gelu_p_kernel(
                 nc.scalar.activation(y_h[:, s0 : s0 + n], acc[:], GELU)
             y.append(y_h)
 
-        W = 256
-        parts = [(0, 0), (0, W), (1, 0), (1, W)]
-        ab, lo, spread, rise = {}, {}, {}, {}
+        squares = [slice(j * P, (j + 1) * P) for j in range(V // P)]
+        per_part = PART // P
+        diff_banks = [(0, 1, 2, 3), (5, 6, 0, 1)]
+        spread_banks = [4, 7, 2, 3]
+        first, second, diff, lo, spread, rise, step = {}, {}, {}, {}, {}, {}, {}
 
-        def nbr(k, i):
-            h, v0 = parts[k]
-            return y[h][:].indirect(pos_t[i][:, v0 // LANES : (v0 + W) // LANES])
+        def part_cols(k):
+            return slice(PART * (k % 2), PART * (k % 2 + 1))
 
-        def fetch(k, i):
-            if i == 0:
-                ab[k] = keep.tile([P, 2, W], F32, name=f"ab{k}", tag=f"hold{k - 2}")
-            nc.vector.tensor_copy(ab[k][:, i, :], nbr(k, i))
+        def neighbours(k, i):
+            v0 = PART * (k % 2)
+            return y[k // 2][:].indirect(pos_t[i][:, v0 // LANES : (v0 + PART) // LANES])
 
-        diff_banks = [(0, 1), (3, 4), (5, 6), (1, 3)]
-        spread_banks = [2, 7, 0, 4]
+        def fetch_first(h, tag):
+            first[h] = keep.tile([P, V], F32, name=f"first{h}", tag=tag)
+            nc.vector.tensor_copy(first[h][:], y[h][:].indirect(pos_t[0][:]))
+            neg = keep.tile([P, V], F32, name=f"neg{h}")
+            nc.scalar.activation(neg[:], first[h][:], COPY, scale=-1.0)
+            for j, c in enumerate(squares):
+                diff[h, j] = psum.tile([P, P], F32, name=f"diff{h}_{j}", tag=f"bank{diff_banks[h][j]}")
+                nc.tensor.matmul(diff[h, j][:], neg[:, c], ident[:], is_transpose=True, start=True, stop=False)
 
-        def make_spread(k):
-            neg = keep.tile([P, W], F32, name=f"neg{k}")
-            nc.scalar.activation(neg[:], ab[k][:, 0, :], COPY, scale=-1.0)
-            blocks = [slice(j * P, (j + 1) * P) for j in range(W // P)]
-            diff = [psum.tile([P, P], F32, name=f"diff{k}_{j}", tag=f"bank{diff_banks[k][j]}") for j in range(W // P)]
-            for j, c in enumerate(blocks):
-                nc.tensor.matmul(diff[j][:], neg[:, c], ident[:], is_transpose=True, start=True, stop=False)
-            for j, c in enumerate(blocks):
-                nc.tensor.matmul(diff[j][:], ab[k][:, 1, c], ident[:], is_transpose=True, start=False, stop=True)
-            turned = keep.tile([P, W], F32, name=f"turned{k}", tag=f"hold{k}")
-            spread[k] = psum.tile([P, W], F32, name=f"spread{k}", tag=f"bank{spread_banks[k]}")
-            for j, c in enumerate(blocks):
-                nc.scalar.activation(turned[:, c], diff[j][:], ABS)
-            for j, c in enumerate(blocks):
-                nc.tensor.transpose(spread[k][:, c], turned[:, c], ident[:])
+        def fetch_second(h, tag):
+            second[h] = keep.tile([P, V], F32, name=f"second{h}", tag=tag)
+            for k in (2 * h, 2 * h + 1):
+                nc.vector.tensor_copy(second[h][:, part_cols(k)], neighbours(k, 1))
+                mine = range(per_part * (k % 2), per_part * (k % 2 + 1))
+                for j in mine:
+                    nc.tensor.matmul(
+                        diff[h, j][:], second[h][:, squares[j]], ident[:], is_transpose=True, start=False, stop=True
+                    )
+                turned = keep.tile([P, PART], F32, name=f"turned{k}")
+                spread[k] = psum.tile([P, PART], F32, name=f"spread{k}", tag=f"bank{spread_banks[k]}")
+                for i, j in enumerate(mine):
+                    nc.scalar.activation(turned[:, squares[i]], diff[h, j][:], ABS)
+                for i in range(per_part):
+                    nc.tensor.transpose(spread[k][:, squares[i]], turned[:, squares[i]], ident[:])
 
-        def make_lo(k):
-            lo[k] = keep.tile([P, W], F32, name=f"lo{k}", tag="rise1" if k == 2 else f"lo{k}")
-            nc.vector.tensor_tensor(lo[k][:], ab[k][:, 0, :], ab[k][:, 1, :], MIN)
+        def make_lo(k, tag):
+            lo[k] = keep.tile([P, PART], F32, name=f"lo{k}", tag=tag)
+            nc.vector.tensor_tensor(lo[k][:], first[k // 2][:, part_cols(k)], second[k // 2][:, part_cols(k)], MIN)
 
         def make_rise(k):
-            rise[k] = keep.tile([P, W], F32, name=f"rise{k}")
-            nc.vector.tensor_tensor(rise[k][:], nbr(k, 2), lo[k][:], SUB)
-
-        step = {}
+            rise[k] = keep.tile([P, PART], F32, name=f"rise{k}")
+            nc.vector.tensor_tensor(rise[k][:], neighbours(k, 2), lo[k][:], SUB)
 
         def make_step(k):
-            step[k] = keep.tile([P, W], F32, name=f"step{k}")
+            step[k] = keep.tile([P, PART], F32, name=f"step{k}")
             nc.vector.scalar_tensor_tensor(step[k][:], rise[k][:], 0.0, spread[k][:], MAX, MIN)
 
-        def finish(k, engine, queue):
-            h, v0 = parts[k]
-            med = keep.tile([P, W], F32, name=f"med{k}")
+        def finish(k, engine, queue, tag):
+            med = keep.tile([P, PART], F32, name=f"med{k}", tag=tag)
             engine.tensor_tensor(med[:], lo[k][:], step[k][:], ADD)
-            queue.dma_start(out[h * P : (h + 1) * P, v0 : v0 + W], med[:])
+            queue.dma_start(out[P * (k // 2) : P * (k // 2 + 1), part_cols(k)], med[:])
 
+        fetch_first(0, "first0")
+        fetch_second(0, "second0")
         for k in (0, 1):
-            fetch(k, 0)
-            fetch(k, 1)
-            make_spread(k)
-        for k in (0, 1):
-            make_lo(k)
+            make_lo(k, f"lo{k}")
         for k in (0, 1):
             make_rise(k)
-        for k in (0, 1):
-            make_step(k)
-            finish(k, nc.gpsimd, nc.sync)
-            fetch(k + 2, 0)
-            fetch(k + 2, 1)
-            make_spread(k + 2)
-        for k in (2, 3):
-            make_lo(k)
+        make_step(0)
+        finish(0, nc.gpsimd, nc.sync, "med0")
+        fetch_first(1, "turned0")
+        make_step(1)
+        finish(1, nc.gpsimd, nc.sync, "med1")
+        fetch_second(1, "turned1")
+        make_lo(2, "rise1")
+        make_lo(3, "lo3")
         for k in (2, 3):
             make_rise(k)
         for k in (2, 3):
             make_step(k)
-        finish(2, nc.vector, nc.sync)
-        finish(3, nc.vector, nc.scalar)
+        finish(2, nc.vector, nc.sync, "turned3")
+        finish(3, nc.vector, nc.scalar, "med3")

@@ -16,6 +16,7 @@ FP8X4 = mybir.dt.float8_e4m3fn_x4
 GELU = mybir.ActivationFunctionType.Gelu_apprx_tanh
 COPY = mybir.ActivationFunctionType.Copy
 ABS = mybir.ActivationFunctionType.Abs
+RELU = mybir.ActivationFunctionType.Relu
 MAX = mybir.AluOpType.max
 MIN = mybir.AluOpType.min
 ADD = mybir.AluOpType.add
@@ -114,76 +115,94 @@ def tile_picked_median_gelu_p_kernel(
 
         squares = [slice(j * P, (j + 1) * P) for j in range(V // P)]
         per_part = PART // P
-        diff_banks = [(0, 1, 2, 3), (5, 6, 0, 1)]
-        spread_banks = [4, 7, 2, 3]
-        first, second, diff, lo, spread, rise, step = {}, {}, {}, {}, {}, {}, {}
 
         def part_cols(k):
             return slice(PART * (k % 2), PART * (k % 2 + 1))
 
-        def neighbours(k, i):
-            v0 = PART * (k % 2)
-            return y[k // 2][:].indirect(pos_t[i][:, v0 // LANES : (v0 + PART) // LANES])
+        def part_squares(k):
+            return range(per_part * (k % 2), per_part * (k % 2 + 1))
 
-        def fetch_first(h, tag):
-            first[h] = keep.tile([P, V], F32, name=f"first{h}", tag=tag)
-            nc.vector.tensor_copy(first[h][:], y[h][:].indirect(pos_t[0][:]))
-            neg = keep.tile([P, V], F32, name=f"neg{h}")
-            nc.scalar.activation(neg[:], first[h][:], COPY, scale=-1.0)
+        def gather(dst, h, i, v0, n):
+            nc.vector.tensor_copy(dst, y[h][:].indirect(pos_t[i][:, v0 // LANES : (v0 + n) // LANES]))
+
+        def transpose_add(dst, src, start, stop):
+            nc.tensor.matmul(dst, src, ident[:], is_transpose=True, start=start, stop=stop)
+
+        def open_difference(h, a, banks, tag):
+            neg = keep.tile([P, V], F32, name=f"neg{h}", tag=tag)
+            for k in (0, 1):
+                nc.scalar.activation(neg[:, part_cols(k)], a[:, part_cols(k)], COPY, scale=-1.0)
+            diff = []
             for j, c in enumerate(squares):
-                diff[h, j] = psum.tile([P, P], F32, name=f"diff{h}_{j}", tag=f"bank{diff_banks[h][j]}")
-                nc.tensor.matmul(diff[h, j][:], neg[:, c], ident[:], is_transpose=True, start=True, stop=False)
+                diff.append(psum.tile([P, P], F32, name=f"diff{h}_{j}", tag=f"bank{banks[j]}"))
+                transpose_add(diff[j][:], neg[:, c], True, False)
+            return diff
 
-        def fetch_second(h, tag):
-            second[h] = keep.tile([P, V], F32, name=f"second{h}", tag=tag)
-            for k in (2 * h, 2 * h + 1):
-                nc.vector.tensor_copy(second[h][:, part_cols(k)], neighbours(k, 1))
-                mine = range(per_part * (k % 2), per_part * (k % 2 + 1))
-                for j in mine:
-                    nc.tensor.matmul(
-                        diff[h, j][:], second[h][:, squares[j]], ident[:], is_transpose=True, start=False, stop=True
-                    )
-                turned = keep.tile([P, PART], F32, name=f"turned{k}")
-                spread[k] = psum.tile([P, PART], F32, name=f"spread{k}", tag=f"bank{spread_banks[k]}")
-                for i, j in enumerate(mine):
-                    nc.scalar.activation(turned[:, squares[i]], diff[h, j][:], ABS)
-                for i in range(per_part):
-                    nc.tensor.transpose(spread[k][:, squares[i]], turned[:, squares[i]], ident[:])
+        def close_difference(k, diff, b, func):
+            turned = [keep.tile([P, P], F32, name=f"turned{k}_{i}", tag=f"turned{k}_{i}") for i in range(per_part)]
+            for i, j in enumerate(part_squares(k)):
+                transpose_add(diff[j][:], b[:, squares[i]], False, True)
+            for i, j in enumerate(part_squares(k)):
+                nc.scalar.activation(turned[i][:], diff[j][:], func)
+            return turned
 
-        def make_lo(k, tag):
-            lo[k] = keep.tile([P, PART], F32, name=f"lo{k}", tag=tag)
-            nc.vector.tensor_tensor(lo[k][:], first[k // 2][:, part_cols(k)], second[k // 2][:, part_cols(k)], MIN)
-
-        def make_rise(k):
-            rise[k] = keep.tile([P, PART], F32, name=f"rise{k}")
-            nc.vector.tensor_tensor(rise[k][:], neighbours(k, 2), lo[k][:], SUB)
-
-        def make_step(k):
-            step[k] = keep.tile([P, PART], F32, name=f"step{k}")
-            nc.vector.scalar_tensor_tensor(step[k][:], rise[k][:], 0.0, spread[k][:], MAX, MIN)
-
-        def finish(k, engine, queue, tag):
-            med = keep.tile([P, PART], F32, name=f"med{k}", tag=tag)
-            engine.tensor_tensor(med[:], lo[k][:], step[k][:], ADD)
+        def store(k, med, queue):
             queue.dma_start(out[P * (k // 2) : P * (k // 2 + 1), part_cols(k)], med[:])
 
-        fetch_first(0, "first0")
-        fetch_second(0, "second0")
+        a0 = keep.tile([P, V], F32, name="a0")
+        gather(a0[:], 0, 0, 0, V)
+        diff0 = open_difference(0, a0, (0, 1, 2, 3), "neg0")
+        b0 = keep.tile([P, V], F32, name="b0")
+        gather(b0[:], 0, 1, 0, V)
+        spread = []
         for k in (0, 1):
-            make_lo(k, f"lo{k}")
+            turned = close_difference(k, diff0, b0[:, part_cols(k)], ABS)
+            spread.append(psum.tile([P, PART], F32, name=f"spread{k}", tag=f"bank{(4, 7)[k]}"))
+            for i in range(per_part):
+                nc.tensor.transpose(spread[k][:, squares[i]], turned[i][:], ident[:])
+        c0 = [keep.tile([P, PART], F32, name=f"c0_{k}", tag=f"c0_{k}") for k in (0, 1)]
         for k in (0, 1):
-            make_rise(k)
-        make_step(0)
-        finish(0, nc.gpsimd, nc.sync, "med0")
-        fetch_first(1, "turned0")
-        make_step(1)
-        finish(1, nc.gpsimd, nc.sync, "med1")
-        fetch_second(1, "turned1")
-        make_lo(2, "rise1")
-        make_lo(3, "lo3")
-        for k in (2, 3):
-            make_rise(k)
-        for k in (2, 3):
-            make_step(k)
-        finish(2, nc.vector, nc.sync, "turned3")
-        finish(3, nc.vector, nc.scalar, "med3")
+            gather(c0[k][:], 0, 2, PART * k, PART)
+        lo0 = [keep.tile([P, PART], F32, name=f"lo{k}") for k in (0, 1)]
+        rise = [keep.tile([P, PART], F32, name=f"rise{k}") for k in (0, 1)]
+        for k in (0, 1):
+            nc.vector.tensor_tensor(lo0[k][:], a0[:, part_cols(k)], b0[:, part_cols(k)], MIN)
+        for k in (0, 1):
+            nc.gpsimd.tensor_tensor(rise[k][:], c0[k][:], lo0[k][:], SUB)
+
+        a1 = keep.tile([P, V], F32, name="a1")
+        gather(a1[:], 1, 0, 0, V)
+        a1_bank = psum.tile([P, V], F32, name="a1_bank", tag="bank3")
+        for c in squares:
+            nc.tensor.transpose(a1_bank[:, c], a1[:, c], ident[:])
+        diff1 = open_difference(1, a1, (6, 5, 0, 1), "turned0_0")
+        a1_turned = keep.tile([P, V], F32, name="a1_turned")
+        nc.scalar.activation(a1_turned[:], a1_bank[:], COPY)
+
+        b1, hi = [], []
+        for k in (0, 1):
+            step = keep.tile([P, PART], F32, name=f"step{k}", tag=f"step{k}")
+            nc.vector.scalar_tensor_tensor(step[:], rise[k][:], 0.0, spread[k][:], MAX, MIN)
+            med = keep.tile([P, PART], F32, name=f"med{k}")
+            nc.gpsimd.tensor_tensor(med[:], lo0[k][:], step[:], ADD)
+            store(k, med, nc.sync)
+            b1.append(keep.tile([P, PART], F32, name=f"b1_{k}", tag=f"turned{k}_1"))
+            gather(b1[k][:], 1, 1, PART * k, PART)
+            excess = close_difference(2 + k, diff1, b1[k], RELU)
+            hi.append(psum.tile([P, PART], F32, name=f"hi{k}", tag=f"bank{(2, 4)[k]}"))
+            for i, j in enumerate(part_squares(k)):
+                transpose_add(hi[k][:, squares[i]], a1_turned[:, squares[j]], True, False)
+                transpose_add(hi[k][:, squares[i]], excess[i][:], False, True)
+
+        c1 = keep.tile([P, V], F32, name="c1", tag="step0")
+        gather(c1[:], 1, 2, 0, V)
+        lo1 = keep.tile([P, V], F32, name="lo1_half", tag="step1")
+        for k in (0, 1):
+            nc.vector.tensor_tensor(lo1[:, part_cols(k)], a1[:, part_cols(k)], b1[k][:], MIN)
+        above = keep.tile([P, V], F32, name="above")
+        for k in (0, 1):
+            nc.vector.tensor_tensor(above[:, part_cols(k)], c1[:, part_cols(k)], lo1[:, part_cols(k)], MAX)
+        for k in (0, 1):
+            med = keep.tile([P, PART], F32, name=f"med{2 + k}")
+            nc.vector.tensor_tensor(med[:], above[:, part_cols(k)], hi[k][:], MIN)
+            store(2 + k, med, (nc.sync, nc.scalar)[k])

@@ -113,14 +113,13 @@ def tile_picked_median_gelu_p_kernel(
                 nc.scalar.activation(y_h[:, s0 : s0 + n], acc[:], GELU)
             y.append(y_h)
 
-        squares = [slice(j * P, (j + 1) * P) for j in range(V // P)]
         per_part = PART // P
+        squares = [slice(i * P, (i + 1) * P) for i in range(per_part)]
+
+        placed = ctx.enter_context(tc.tile_pool(name="placed", bufs=1))
 
         def part_cols(k):
             return slice(PART * (k % 2), PART * (k % 2 + 1))
-
-        def part_squares(k):
-            return range(per_part * (k % 2), per_part * (k % 2 + 1))
 
         def gather(dst, h, i, v0, n):
             nc.vector.tensor_copy(dst, y[h][:].indirect(pos_t[i][:, v0 // LANES : (v0 + n) // LANES]))
@@ -128,81 +127,98 @@ def tile_picked_median_gelu_p_kernel(
         def transpose_add(dst, src, start, stop):
             nc.tensor.matmul(dst, src, ident[:], is_transpose=True, start=start, stop=stop)
 
-        def open_difference(h, a, banks, tag):
-            neg = keep.tile([P, V], F32, name=f"neg{h}", tag=tag)
-            for k in (0, 1):
-                nc.scalar.activation(neg[:, part_cols(k)], a[:, part_cols(k)], COPY, scale=-1.0)
+        def open_difference(k, a, banks):
             diff = []
-            for j, c in enumerate(squares):
-                diff.append(psum.tile([P, P], F32, name=f"diff{h}_{j}", tag=f"bank{banks[j]}"))
-                transpose_add(diff[j][:], neg[:, c], True, False)
+            for i, c in enumerate(squares):
+                if k == 1:
+                    neg = placed.tile([P, P], F32, name=f"neg{k}_{i}", offset=2048 * i + 1024)
+                else:
+                    neg = keep.tile([P, P], F32, name=f"neg{k}_{i}", tag=f"neg{k}_{i}")
+                nc.scalar.activation(neg[:], a[:, c], COPY, scale=-1.0)
+                diff.append(psum.tile([P, P], F32, name=f"diff{k}_{i}", tag=f"bank{banks[i]}"))
+                transpose_add(diff[i][:], neg[:], True, False)
             return diff
 
         def close_difference(k, diff, b, func):
-            turned = [keep.tile([P, P], F32, name=f"turned{k}_{i}", tag=f"turned{k}_{i}") for i in range(per_part)]
-            for i, j in enumerate(part_squares(k)):
-                transpose_add(diff[j][:], b[:, squares[i]], False, True)
-            for i, j in enumerate(part_squares(k)):
-                nc.scalar.activation(turned[i][:], diff[j][:], func)
+            turned = [keep.tile([P, P], F32, name=f"turned{k}_0", tag=f"turned{k}_0")]
+            if k < 2:
+                turned.append(placed.tile([P, P], F32, name=f"turned{k}_1", offset=2048 * k))
+            else:
+                turned.append(keep.tile([P, P], F32, name=f"turned{k}_1"))
+            for i, c in enumerate(squares):
+                transpose_add(diff[i][:], b[:, c], False, True)
+            for i in range(per_part):
+                nc.scalar.activation(turned[i][:], diff[i][:], func)
             return turned
+
+        def open_upper(k, a, bank):
+            there = psum.tile([P, PART], F32, name=f"there{k}", tag=f"bank{bank}")
+            for c in squares:
+                nc.tensor.transpose(there[:, c], a[:, c], ident[:])
+            a_turned = keep.tile([P, PART], F32, name=f"a_turned{k}")
+            nc.scalar.activation(a_turned[:], there[:], COPY)
+            upper = psum.tile([P, PART], F32, name=f"upper{k}", tag=f"bank{bank}")
+            for i, c in enumerate(squares):
+                transpose_add(upper[:, c], a_turned[:, c], i == 0, False)
+            return upper
 
         def store(k, med, queue):
             queue.dma_start(out[P * (k // 2) : P * (k // 2 + 1), part_cols(k)], med[:])
 
         a0 = keep.tile([P, V], F32, name="a0")
         gather(a0[:], 0, 0, 0, V)
-        diff0 = open_difference(0, a0, (0, 1, 2, 3), "neg0")
+        diff = {0: open_difference(0, a0[:, part_cols(0)], (0, 1)), 1: open_difference(1, a0[:, part_cols(1)], (2, 3))}
         b0 = keep.tile([P, V], F32, name="b0")
         gather(b0[:], 0, 1, 0, V)
         spread = []
         for k in (0, 1):
-            turned = close_difference(k, diff0, b0[:, part_cols(k)], ABS)
+            turned = close_difference(k, diff[k], b0[:, part_cols(k)], ABS)
             spread.append(psum.tile([P, PART], F32, name=f"spread{k}", tag=f"bank{(4, 7)[k]}"))
-            for i in range(per_part):
-                nc.tensor.transpose(spread[k][:, squares[i]], turned[i][:], ident[:])
-        c0 = [keep.tile([P, PART], F32, name=f"c0_{k}", tag=f"c0_{k}") for k in (0, 1)]
-        for k in (0, 1):
-            gather(c0[k][:], 0, 2, PART * k, PART)
-        lo0 = [keep.tile([P, PART], F32, name=f"lo{k}") for k in (0, 1)]
-        rise = [keep.tile([P, PART], F32, name=f"rise{k}") for k in (0, 1)]
-        for k in (0, 1):
-            nc.vector.tensor_tensor(lo0[k][:], a0[:, part_cols(k)], b0[:, part_cols(k)], MIN)
-        for k in (0, 1):
-            nc.gpsimd.tensor_tensor(rise[k][:], c0[k][:], lo0[k][:], SUB)
+            for i, c in enumerate(squares):
+                nc.tensor.transpose(spread[k][:, c], turned[i][:], ident[:])
 
-        a1 = keep.tile([P, V], F32, name="a1")
-        gather(a1[:], 1, 0, 0, V)
-        a1_bank = psum.tile([P, V], F32, name="a1_bank", tag="bank3")
-        for c in squares:
-            nc.tensor.transpose(a1_bank[:, c], a1[:, c], ident[:])
-        diff1 = open_difference(1, a1, (6, 5, 0, 1), "turned0_0")
-        a1_turned = keep.tile([P, V], F32, name="a1_turned")
-        nc.scalar.activation(a1_turned[:], a1_bank[:], COPY)
+        a1, upper = {}, {}
 
-        b1, hi = [], []
+        def fetch_a1(k, tag, diff_banks, upper_bank):
+            a1[k] = keep.tile([P, PART], F32, name=f"a1_{k}", tag=tag)
+            gather(a1[k][:], 1, 0, PART * (k % 2), PART)
+            diff[k] = open_difference(k, a1[k], diff_banks)
+            upper[k] = open_upper(k, a1[k], upper_bank)
+
+        fetch_a1(2, "a1_2", (0, 1), 2)
+        lo0 = keep.tile([P, V], F32, name="lo0", tag="neg0_1")
+        for k in (0, 1):
+            nc.vector.tensor_tensor(lo0[:, part_cols(k)], a0[:, part_cols(k)], b0[:, part_cols(k)], MIN)
+        rise = []
+        for k in (0, 1):
+            c0 = placed.tile([P, PART], F32, name=f"c0_{k}", offset=2048 * k + 512)
+            gather(c0[:], 0, 2, PART * k, PART)
+            rise.append(keep.tile([P, PART], F32, name=f"rise{k}"))
+            nc.gpsimd.tensor_tensor(rise[k][:], c0[:], lo0[:, part_cols(k)], SUB)
+        fetch_a1(3, "turned0_0", (5, 6), 3)
+
+        b1 = {}
         for k in (0, 1):
             step = keep.tile([P, PART], F32, name=f"step{k}", tag=f"step{k}")
             nc.vector.scalar_tensor_tensor(step[:], rise[k][:], 0.0, spread[k][:], MAX, MIN)
             med = keep.tile([P, PART], F32, name=f"med{k}")
-            nc.gpsimd.tensor_tensor(med[:], lo0[k][:], step[:], ADD)
+            nc.gpsimd.tensor_tensor(med[:], lo0[:, part_cols(k)], step[:], ADD)
             store(k, med, nc.sync)
-            b1.append(keep.tile([P, PART], F32, name=f"b1_{k}", tag=f"turned{k}_1"))
-            gather(b1[k][:], 1, 1, PART * k, PART)
-            excess = close_difference(2 + k, diff1, b1[k], RELU)
-            hi.append(psum.tile([P, PART], F32, name=f"hi{k}", tag=f"bank{(2, 4)[k]}"))
-            for i, j in enumerate(part_squares(k)):
-                transpose_add(hi[k][:, squares[i]], a1_turned[:, squares[j]], True, False)
-                transpose_add(hi[k][:, squares[i]], excess[i][:], False, True)
+            b1[2 + k] = placed.tile([P, PART], F32, name=f"b1_{k}", offset=2048 * k)
+            gather(b1[2 + k][:], 1, 1, PART * k, PART)
+            excess = close_difference(2 + k, diff[2 + k], b1[2 + k], RELU)
+            for i, c in enumerate(squares):
+                transpose_add(upper[2 + k][:, c], excess[i][:], False, i == per_part - 1)
 
         c1 = keep.tile([P, V], F32, name="c1", tag="step0")
         gather(c1[:], 1, 2, 0, V)
-        lo1 = keep.tile([P, V], F32, name="lo1_half", tag="step1")
-        for k in (0, 1):
-            nc.vector.tensor_tensor(lo1[:, part_cols(k)], a1[:, part_cols(k)], b1[k][:], MIN)
+        lo1 = keep.tile([P, V], F32, name="lo1", tag="step1")
+        for k in (2, 3):
+            nc.vector.tensor_tensor(lo1[:, part_cols(k)], a1[k][:], b1[k][:], MIN)
         above = keep.tile([P, V], F32, name="above")
-        for k in (0, 1):
+        for k in (2, 3):
             nc.vector.tensor_tensor(above[:, part_cols(k)], c1[:, part_cols(k)], lo1[:, part_cols(k)], MAX)
-        for k in (0, 1):
-            med = keep.tile([P, PART], F32, name=f"med{2 + k}")
-            nc.vector.tensor_tensor(med[:], above[:, part_cols(k)], hi[k][:], MIN)
-            store(2 + k, med, (nc.sync, nc.scalar)[k])
+        for k in (2, 3):
+            med = keep.tile([P, PART], F32, name=f"med{k}")
+            nc.vector.tensor_tensor(med[:], above[:, part_cols(k)], upper[k][:], MIN)
+            store(k, med, (nc.sync, nc.scalar)[k % 2])

@@ -116,35 +116,25 @@ def tile_picked_median_gelu_p_kernel(
         per_part = PART // P
         squares = [slice(i * P, (i + 1) * P) for i in range(per_part)]
 
-        placed = ctx.enter_context(tc.tile_pool(name="placed", bufs=1))
-
         def part_cols(k):
             return slice(PART * (k % 2), PART * (k % 2 + 1))
 
-        def gather(dst, h, i, v0, n):
-            nc.vector.tensor_copy(dst, y[h][:].indirect(pos_t[i][:, v0 // LANES : (v0 + n) // LANES]))
+        def neighbours(h, i, v0, n):
+            return y[h][:].indirect(pos_t[i][:, v0 // LANES : (v0 + n) // LANES])
 
         def transpose_add(dst, src, start, stop):
             nc.tensor.matmul(dst, src, ident[:], is_transpose=True, start=start, stop=stop)
 
-        def open_difference(k, a, banks):
+        def open_difference(k, a, neg, banks):
+            nc.scalar.activation(neg, a, COPY, scale=-1.0)
             diff = []
             for i, c in enumerate(squares):
-                if k == 1:
-                    neg = placed.tile([P, P], F32, name=f"neg{k}_{i}", offset=2048 * i + 1024)
-                else:
-                    neg = keep.tile([P, P], F32, name=f"neg{k}_{i}", tag=f"neg{k}_{i}")
-                nc.scalar.activation(neg[:], a[:, c], COPY, scale=-1.0)
                 diff.append(psum.tile([P, P], F32, name=f"diff{k}_{i}", tag=f"bank{banks[i]}"))
-                transpose_add(diff[i][:], neg[:], True, False)
+                transpose_add(diff[i][:], neg[:, c], True, False)
             return diff
 
         def close_difference(k, diff, b, func):
-            turned = [keep.tile([P, P], F32, name=f"turned{k}_0", tag=f"turned{k}_0")]
-            if k < 2:
-                turned.append(placed.tile([P, P], F32, name=f"turned{k}_1", offset=2048 * k))
-            else:
-                turned.append(keep.tile([P, P], F32, name=f"turned{k}_1"))
+            turned = [keep.tile([P, P], F32, name=f"turned{k}_{i}", tag=f"turned{k}_{i}") for i in range(per_part)]
             for i, c in enumerate(squares):
                 transpose_add(diff[i][:], b[:, c], False, True)
             for i in range(per_part):
@@ -166,10 +156,13 @@ def tile_picked_median_gelu_p_kernel(
             queue.dma_start(out[P * (k // 2) : P * (k // 2 + 1), part_cols(k)], med[:])
 
         a0 = keep.tile([P, V], F32, name="a0")
-        gather(a0[:], 0, 0, 0, V)
-        diff = {0: open_difference(0, a0[:, part_cols(0)], (0, 1)), 1: open_difference(1, a0[:, part_cols(1)], (2, 3))}
+        nc.vector.tensor_copy(a0[:], neighbours(0, 0, 0, V))
+        diff = {}
+        for k in (0, 1):
+            neg = keep.tile([P, PART], F32, name=f"neg{k}", tag=f"neg{k}")
+            diff[k] = open_difference(k, a0[:, part_cols(k)], neg[:], (2 * k, 2 * k + 1))
         b0 = keep.tile([P, V], F32, name="b0")
-        gather(b0[:], 0, 1, 0, V)
+        nc.vector.tensor_copy(b0[:], neighbours(0, 1, 0, V))
         spread = []
         for k in (0, 1):
             turned = close_difference(k, diff[k], b0[:, part_cols(k)], ABS)
@@ -177,44 +170,42 @@ def tile_picked_median_gelu_p_kernel(
             for i, c in enumerate(squares):
                 nc.tensor.transpose(spread[k][:, c], turned[i][:], ident[:])
 
-        a1, upper = {}, {}
+        a1 = keep.tile([P, V], F32, name="a1")
+        nc.vector.tensor_copy(a1[:], neighbours(1, 0, 0, V))
+        neg1 = keep.tile([P, V], F32, name="neg_half1", tag="turned0_0")
+        upper = {}
+        for k, diff_banks, upper_bank in ((2, (0, 1), 2), (3, (5, 6), 3)):
+            diff[k] = open_difference(k, a1[:, part_cols(k)], neg1[:, part_cols(k)], diff_banks)
+            upper[k] = open_upper(k, a1[:, part_cols(k)], upper_bank)
 
-        def fetch_a1(k, tag, diff_banks, upper_bank):
-            a1[k] = keep.tile([P, PART], F32, name=f"a1_{k}", tag=tag)
-            gather(a1[k][:], 1, 0, PART * (k % 2), PART)
-            diff[k] = open_difference(k, a1[k], diff_banks)
-            upper[k] = open_upper(k, a1[k], upper_bank)
-
-        fetch_a1(2, "a1_2", (0, 1), 2)
-        lo0 = keep.tile([P, V], F32, name="lo0", tag="neg0_1")
+        lo0 = keep.tile([P, V], F32, name="lo0", tag="neg0")
         for k in (0, 1):
             nc.vector.tensor_tensor(lo0[:, part_cols(k)], a0[:, part_cols(k)], b0[:, part_cols(k)], MIN)
-        rise = []
+        rise = keep.tile([P, V], F32, name="rise")
         for k in (0, 1):
-            c0 = placed.tile([P, PART], F32, name=f"c0_{k}", offset=2048 * k + 512)
-            gather(c0[:], 0, 2, PART * k, PART)
-            rise.append(keep.tile([P, PART], F32, name=f"rise{k}"))
-            nc.gpsimd.tensor_tensor(rise[k][:], c0[:], lo0[:, part_cols(k)], SUB)
-        fetch_a1(3, "turned0_0", (5, 6), 3)
+            nc.vector.tensor_tensor(rise[:, part_cols(k)], neighbours(0, 2, PART * k, PART), lo0[:, part_cols(k)], SUB)
 
-        b1 = {}
-        for k in (0, 1):
+        def finish_on_gpsimd(k):
             step = keep.tile([P, PART], F32, name=f"step{k}", tag=f"step{k}")
-            nc.vector.scalar_tensor_tensor(step[:], rise[k][:], 0.0, spread[k][:], MAX, MIN)
+            nc.vector.scalar_tensor_tensor(step[:], rise[:, part_cols(k)], 0.0, spread[k][:], MAX, MIN)
             med = keep.tile([P, PART], F32, name=f"med{k}")
             nc.gpsimd.tensor_tensor(med[:], lo0[:, part_cols(k)], step[:], ADD)
             store(k, med, nc.sync)
-            b1[2 + k] = placed.tile([P, PART], F32, name=f"b1_{k}", offset=2048 * k)
-            gather(b1[2 + k][:], 1, 1, PART * k, PART)
-            excess = close_difference(2 + k, diff[2 + k], b1[2 + k], RELU)
-            for i, c in enumerate(squares):
-                transpose_add(upper[2 + k][:, c], excess[i][:], False, i == per_part - 1)
 
-        c1 = keep.tile([P, V], F32, name="c1", tag="step0")
-        gather(c1[:], 1, 2, 0, V)
+        finish_on_gpsimd(0)
+        b1 = keep.tile([P, V], F32, name="b1", tag="turned0_1")
+        nc.vector.tensor_copy(b1[:], neighbours(1, 1, 0, V))
+        for k in (2, 3):
+            excess = close_difference(k, diff[k], b1[:, part_cols(k)], RELU)
+            for i, c in enumerate(squares):
+                transpose_add(upper[k][:, c], excess[i][:], False, i == per_part - 1)
+        finish_on_gpsimd(1)
+        c1 = keep.tile([P, V], F32, name="c1", tag="turned1_1")
+        nc.vector.tensor_copy(c1[:], neighbours(1, 2, 0, V))
+
         lo1 = keep.tile([P, V], F32, name="lo1", tag="step1")
         for k in (2, 3):
-            nc.vector.tensor_tensor(lo1[:, part_cols(k)], a1[k][:], b1[k][:], MIN)
+            nc.vector.tensor_tensor(lo1[:, part_cols(k)], a1[:, part_cols(k)], b1[:, part_cols(k)], MIN)
         above = keep.tile([P, V], F32, name="above")
         for k in (2, 3):
             nc.vector.tensor_tensor(above[:, part_cols(k)], c1[:, part_cols(k)], lo1[:, part_cols(k)], MAX)

@@ -204,12 +204,11 @@ def tile_picked_median_gelu_p_kernel(
         nc.vector.tensor_copy(c1[:], neighbours(1, 2, 0, V))
 
         lo1 = keep.tile([P, V], F32, name="lo1", tag="step1")
+        nc.vector.tensor_tensor(lo1[:], a1[:], b1[:], MIN)
+        below = keep.tile([P, V], F32, name="below")
         for k in (2, 3):
-            nc.vector.tensor_tensor(lo1[:, part_cols(k)], a1[:, part_cols(k)], b1[:, part_cols(k)], MIN)
-        above = keep.tile([P, V], F32, name="above")
-        for k in (2, 3):
-            nc.vector.tensor_tensor(above[:, part_cols(k)], c1[:, part_cols(k)], lo1[:, part_cols(k)], MAX)
+            nc.vector.tensor_tensor(below[:, part_cols(k)], c1[:, part_cols(k)], upper[k][:], MIN)
         for k in (2, 3):
             med = keep.tile([P, PART], F32, name=f"med{k}")
-            nc.vector.tensor_tensor(med[:], above[:, part_cols(k)], upper[k][:], MIN)
+            nc.vector.tensor_tensor(med[:], below[:, part_cols(k)], lo1[:, part_cols(k)], MAX)
             store(k, med, (nc.sync, nc.scalar)[k % 2])

@@ -211,4 +211,4 @@ def tile_picked_median_gelu_p_kernel(
         for k in (2, 3):
             med = keep.tile([P, PART], F32, name=f"med{k}")
             nc.vector.tensor_tensor(med[:], below[:, part_cols(k)], lo1[:, part_cols(k)], MAX)
-            store(k, med, (nc.sync, nc.scalar)[k % 2])
+            store(k, med, nc.scalar)

@@ -21,6 +21,7 @@ MAX = mybir.AluOpType.max
 MIN = mybir.AluOpType.min
 ADD = mybir.AluOpType.add
 SUB = mybir.AluOpType.subtract
+MULT = mybir.AluOpType.mult
 
 P = 128
 PACK = 4
@@ -28,6 +29,7 @@ LANES = 16
 BLOCKS = K // 32
 ROW0 = P - BLOCKS
 CHUNK = 512
+SPLIT = 96
 PART = 256
 
 
@@ -39,21 +41,31 @@ def tile_picked_median_gelu_p_kernel(
         keep = ctx.enter_context(tc.tile_pool(name="keep", bufs=1))
         psum = ctx.enter_context(tc.psum_pool(name="psum", bufs=1))
 
+        placed = ctx.enter_context(tc.tile_pool(name="placed", bufs=1))
+
         offs_t = keep.tile([P, S // LANES], U16, name="offs_t")
         pos_t = [keep.tile([P, V // LANES], U16, name=f"pos_t{i}") for i in range(3)]
-        scale_table = keep.tile([P, T], U8, name="scale_table", tag="scale_table_then_words", align_bytes=64)
+        scale_table = placed.tile([P, T], U8, name="scale_table", offset=0, align_bytes=64)
         w_rows = w1.rearrange("(p j) m -> p j m", j=PACK)
-        w_raw = [keep.tile([P, PACK, P], F32, name=f"w_raw{h}") for h in range(2)]
+        w_raw = [
+            placed.tile([P, PACK, P], F32, name="w_raw0", offset=4096, align_bytes=64),
+            placed.tile([P, PACK, P], F32, name="w_raw1", offset=0, align_bytes=64),
+        ]
         word_table = keep.tile([P, T], I32, name="word_table", align_bytes=64)
         nc.sync.dma_start(scale_table[ROW0:P, :].bitcast(I32), x_scales[0].bitcast(I32))
         nc.sync.dma_start(offs_t[:], offs)
+        nc.sync.dma_start(word_table[:], x_words[0].rearrange("p n t -> p (n t)").bitcast(I32))
         nc.sync.dma_start(w_raw[0][:], w_rows[:, :, 0 * P : 1 * P])
         nc.sync.dma_start(pos_t[0][:], pos1)
-        nc.sync.dma_start(word_table[:], x_words[0].rearrange("p n t -> p (n t)").bitcast(I32))
-        nc.sync.dma_start(w_raw[1][:], w_rows[:, :, 1 * P : 2 * P])
         nc.sync.dma_start(pos_t[1][:], pos2)
         nc.sync.dma_start(pos_t[2][:], pos3)
         nc.vector.memset(scale_table[0:ROW0, :].bitcast(I32), 0)
+
+        ident = keep.tile([P, P], F32, name="ident")
+        nc.vector.memset(ident[:], 0.0)
+        warm = keep.tile([P, 8], F32, name="warm")
+        nc.scalar.activation(warm[:, 0:1], ident[:, 0:1], GELU)
+        make_identity(nc, ident[:], nomemset=True)
 
         picked_scales = keep.tile([P, S], U8, name="picked_scales", align_bytes=64)
         nc.vector.tensor_copy(picked_scales[:], scale_table[:].indirect(offs_t[:]))
@@ -64,33 +76,40 @@ def tile_picked_median_gelu_p_kernel(
                 x_plane[32 * q : 32 * q + 4, :].bitcast(I32),
                 picked_scales[ROW0 + 4 * q : ROW0 + 4 * q + 4, :].bitcast(I32),
             )
+        nc.scalar.dma_start(w_raw[1][:], w_rows[:, :, 1 * P : 2 * P])
+
+        grouped = [keep.tile([P, P, PACK], BF16, name=f"w_grouped{h}", tag="w_grouped", align_bytes=64) for h in range(2)]
+
+        def walks(h, c0, c1):
+            return (
+                grouped[h][:, c0:c1, :].rearrange("p (c i) j -> p c j i", i=4),
+                w_raw[h][:, :, c0:c1].rearrange("p j (c i) -> p c j i", i=4),
+            )
 
         def quantize_w(h):
-            grouped = keep.tile([P, P, PACK], BF16, name=f"w_grouped{h}", align_bytes=64)
-            nc.vector.tensor_copy(
-                grouped[:].rearrange("p (c i) j -> p c j i", i=4),
-                w_raw[h][:].rearrange("p j (c i) -> p c j i", i=4),
-            )
             codes = keep.tile([P, P], U32, name=f"w_codes{h}", align_bytes=64)
             plane = keep.tile([P, P], U8, name=f"w_plane{h}", align_bytes=64)
             nc.vector.quantize_mx(
-                out=codes[:].bitcast(FP8X4), scales=plane[:], in_=grouped[:].rearrange("p c j -> p (c j)")
+                out=codes[:].bitcast(FP8X4), scales=plane[:], in_=grouped[h][:].rearrange("p c j -> p (c j)")
             )
             return codes, plane
 
-        w_q = [quantize_w(0)]
+        picked = [
+            placed.tile([P, CHUNK], U32, name="picked0", offset=2048, align_bytes=64),
+            placed.tile([P, CHUNK], U32, name="picked1", offset=4096, align_bytes=64),
+        ]
 
-        picked = keep.tile([P, S], U32, name="picked", tag="scale_table_then_words", align_bytes=64)
-        for c in range(S // CHUNK):
+        def gather_words(c):
             cols = slice(c * CHUNK // LANES, (c + 1) * CHUNK // LANES)
-            nc.vector.tensor_copy(
-                picked[:, c * CHUNK : (c + 1) * CHUNK], word_table[:].bitcast(U32).indirect(offs_t[:, cols])
-            )
+            nc.vector.tensor_copy(picked[c][:], word_table[:].bitcast(U32).indirect(offs_t[:, cols]))
 
+        gather_words(0)
+        nc.scalar.copy(*walks(0, 0, SPLIT))
+        nc.gpsimd.tensor_scalar(*walks(0, SPLIT, P), 1.0, 0.0, MULT, ADD)
+        w_q = [quantize_w(0)]
+        gather_words(1)
+        nc.vector.tensor_copy(*walks(1, 0, P))
         w_q.append(quantize_w(1))
-
-        ident = keep.tile([P, P], F32, name="ident", tag="w_grouped0", align_bytes=64)
-        make_identity(nc, ident[:])
 
         pieces = [[(0, CHUNK)] + [(s0, P) for s0 in range(CHUNK, S, P)], [(0, CHUNK), (CHUNK, CHUNK)]]
         y = []
@@ -105,7 +124,7 @@ def tile_picked_median_gelu_p_kernel(
                     out=acc[:],
                     lhsT=codes[:].bitcast(FP8X4),
                     lhsT_scale=plane[:],
-                    rhs=picked[:, s0 : s0 + n].bitcast(FP8X4),
+                    rhs=picked[s0 // CHUNK][:, s0 % CHUNK : s0 % CHUNK + n].bitcast(FP8X4),
                     rhs_scale=x_plane[:, s0 : s0 + n],
                     start=True,
                     stop=True,

@@ -52,7 +52,7 @@ def tile_picked_median_gelu_p_kernel(
             placed.tile([P, PACK, P], F32, name="w_raw1", offset=0, align_bytes=64),
         ]
         word_table = keep.tile([P, T], I32, name="word_table", align_bytes=64)
-        nc.sync.dma_start(scale_table[ROW0:P, :].bitcast(I32), x_scales[0].bitcast(I32))
+        nc.scalar.dma_start(scale_table[ROW0:P, :].bitcast(I32), x_scales[0].bitcast(I32))
         nc.sync.dma_start(offs_t[:], offs)
         nc.sync.dma_start(word_table[:], x_words[0].rearrange("p n t -> p (n t)").bitcast(I32))
         nc.sync.dma_start(w_raw[0][:], w_rows[:, :, 0 * P : 1 * P])

@@ -72,11 +72,11 @@ def tile_picked_median_gelu_p_kernel(
         x_plane = keep.tile([P, S], U8, name="x_plane", align_bytes=64)
         nc.vector.memset(x_plane[:].bitcast(I32), 0)
         for q in range(4):
-            nc.scalar.dma_start(
+            nc.sync.dma_start(
                 x_plane[32 * q : 32 * q + 4, :].bitcast(I32),
                 picked_scales[ROW0 + 4 * q : ROW0 + 4 * q + 4, :].bitcast(I32),
             )
-        nc.scalar.dma_start(w_raw[1][:], w_rows[:, :, 1 * P : 2 * P])
+        nc.sync.dma_start(w_raw[1][:], w_rows[:, :, 1 * P : 2 * P])
 
         grouped = [keep.tile([P, P, PACK], BF16, name=f"w_grouped{h}", tag="w_grouped", align_bytes=64) for h in range(2)]
 

@@ -29,7 +29,7 @@ LANES = 16
 BLOCKS = K // 32
 ROW0 = P - BLOCKS
 CHUNK = 512
-SPLIT = 96
+SPLIT = 64
 PART = 256
 
 

@@ -55,8 +55,8 @@ def tile_picked_median_gelu_p_kernel(
         nc.scalar.dma_start(scale_table[ROW0:P, :].bitcast(I32), x_scales[0].bitcast(I32))
         nc.sync.dma_start(offs_t[:], offs)
         nc.sync.dma_start(word_table[:], x_words[0].rearrange("p n t -> p (n t)").bitcast(I32))
-        nc.sync.dma_start(w_raw[0][:], w_rows[:, :, 0 * P : 1 * P])
         nc.sync.dma_start(pos_t[0][:], pos1)
+        nc.sync.dma_start(w_raw[0][:], w_rows[:, :, 0 * P : 1 * P])
         nc.sync.dma_start(pos_t[1][:], pos2)
         nc.sync.dma_start(pos_t[2][:], pos3)
         nc.vector.memset(scale_table[0:ROW0, :].bitcast(I32), 0)

@@ -1,7 +1,6 @@
 from contextlib import ExitStack
 
 import concourse.mybir as mybir
-from concourse.masks import make_identity
 
 K, T, S, V, N = 512, 4096, 1024, 512, 256
 FLOPS = 2 * K * N * S
@@ -15,12 +14,9 @@ U8 = mybir.dt.uint8
 FP8X4 = mybir.dt.float8_e4m3fn_x4
 GELU = mybir.ActivationFunctionType.Gelu_apprx_tanh
 COPY = mybir.ActivationFunctionType.Copy
-ABS = mybir.ActivationFunctionType.Abs
-RELU = mybir.ActivationFunctionType.Relu
 MAX = mybir.AluOpType.max
 MIN = mybir.AluOpType.min
 ADD = mybir.AluOpType.add
-SUB = mybir.AluOpType.subtract
 MULT = mybir.AluOpType.mult
 
 P = 128
@@ -61,11 +57,9 @@ def tile_picked_median_gelu_p_kernel(
         nc.sync.dma_start(pos_t[2][:], pos3)
         nc.vector.memset(scale_table[0:ROW0, :].bitcast(I32), 0)
 
-        ident = keep.tile([P, P], F32, name="ident")
-        nc.vector.memset(ident[:], 0.0)
-        warm = keep.tile([P, 8], F32, name="warm")
-        nc.scalar.activation(warm[:, 0:1], ident[:, 0:1], GELU)
-        make_identity(nc, ident[:], nomemset=True)
+        warm = keep.tile([P, 16], F32, name="warm")
+        nc.vector.memset(warm[:, 0:1], 0.0)
+        nc.scalar.activation(warm[:, 8:9], warm[:, 0:1], GELU)
 
         picked_scales = keep.tile([P, S], U8, name="picked_scales", align_bytes=64)
         nc.vector.tensor_copy(picked_scales[:], scale_table[:].indirect(offs_t[:]))
@@ -132,102 +126,31 @@ def tile_picked_median_gelu_p_kernel(
                 nc.scalar.activation(y_h[:, s0 : s0 + n], acc[:], GELU)
             y.append(y_h)
 
-        per_part = PART // P
-        squares = [slice(i * P, (i + 1) * P) for i in range(per_part)]
-
-        def part_cols(k):
-            return slice(PART * (k % 2), PART * (k % 2 + 1))
-
         def neighbours(h, i, v0, n):
             return y[h][:].indirect(pos_t[i][:, v0 // LANES : (v0 + n) // LANES])
 
-        def transpose_add(dst, src, start, stop):
-            nc.tensor.matmul(dst, src, ident[:], is_transpose=True, start=start, stop=stop)
+        parts = [slice(v0, v0 + PART) for v0 in range(0, V, PART)]
 
-        def open_difference(k, a, neg, banks):
-            nc.scalar.activation(neg, a, COPY, scale=-1.0)
-            diff = []
-            for i, c in enumerate(squares):
-                diff.append(psum.tile([P, P], F32, name=f"diff{k}_{i}", tag=f"bank{banks[i]}"))
-                transpose_add(diff[i][:], neg[:, c], True, False)
-            return diff
+        def median(h, a, b, c, queue):
+            hi = keep.tile([P, V], F32, name=f"hi{h}")
+            lo = keep.tile([P, V], F32, name=f"lo{h}")
+            below = keep.tile([P, V], F32, name=f"below{h}")
+            med = keep.tile([P, V], F32, name=f"med{h}")
+            nc.vector.tensor_tensor(hi[:], a[:], b[:], MAX)
+            nc.vector.tensor_tensor(lo[:], a[:], b[:], MIN)
+            for v in parts:
+                nc.vector.tensor_tensor(below[:, v], c[:, v], hi[:, v], MIN)
+            for v in parts:
+                nc.vector.tensor_tensor(med[:, v], below[:, v], lo[:, v], MAX)
+                queue.dma_start(out[P * h : P * (h + 1), v], med[:, v])
 
-        def close_difference(k, diff, b, func):
-            turned = [keep.tile([P, P], F32, name=f"turned{k}_{i}", tag=f"turned{k}_{i}") for i in range(per_part)]
-            for i, c in enumerate(squares):
-                transpose_add(diff[i][:], b[:, c], False, True)
-            for i in range(per_part):
-                nc.scalar.activation(turned[i][:], diff[i][:], func)
-            return turned
-
-        def open_upper(k, a, bank):
-            there = psum.tile([P, PART], F32, name=f"there{k}", tag=f"bank{bank}")
-            for c in squares:
-                nc.tensor.transpose(there[:, c], a[:, c], ident[:])
-            a_turned = keep.tile([P, PART], F32, name=f"a_turned{k}")
-            nc.scalar.activation(a_turned[:], there[:], COPY)
-            upper = psum.tile([P, PART], F32, name=f"upper{k}", tag=f"bank{bank}")
-            for i, c in enumerate(squares):
-                transpose_add(upper[:, c], a_turned[:, c], i == 0, False)
-            return upper
-
-        def store(k, med, queue):
-            queue.dma_start(out[P * (k // 2) : P * (k // 2 + 1), part_cols(k)], med[:])
-
-        a0 = keep.tile([P, V], F32, name="a0")
-        nc.vector.tensor_copy(a0[:], neighbours(0, 0, 0, V))
-        diff = {}
-        for k in (0, 1):
-            neg = keep.tile([P, PART], F32, name=f"neg{k}", tag=f"neg{k}")
-            diff[k] = open_difference(k, a0[:, part_cols(k)], neg[:], (2 * k, 2 * k + 1))
-        b0 = keep.tile([P, V], F32, name="b0")
-        nc.vector.tensor_copy(b0[:], neighbours(0, 1, 0, V))
-        spread = []
-        for k in (0, 1):
-            turned = close_difference(k, diff[k], b0[:, part_cols(k)], ABS)
-            spread.append(psum.tile([P, PART], F32, name=f"spread{k}", tag=f"bank{(4, 7)[k]}"))
-            for i, c in enumerate(squares):
-                nc.tensor.transpose(spread[k][:, c], turned[i][:], ident[:])
-
-        a1 = keep.tile([P, V], F32, name="a1")
-        nc.vector.tensor_copy(a1[:], neighbours(1, 0, 0, V))
-        neg1 = keep.tile([P, V], F32, name="neg_half1", tag="turned0_0")
-        upper = {}
-        for k, diff_banks, upper_bank in ((2, (0, 1), 2), (3, (5, 6), 3)):
-            diff[k] = open_difference(k, a1[:, part_cols(k)], neg1[:, part_cols(k)], diff_banks)
-            upper[k] = open_upper(k, a1[:, part_cols(k)], upper_bank)
-
-        lo0 = keep.tile([P, V], F32, name="lo0", tag="neg0")
-        for k in (0, 1):
-            nc.vector.tensor_tensor(lo0[:, part_cols(k)], a0[:, part_cols(k)], b0[:, part_cols(k)], MIN)
-        rise = keep.tile([P, V], F32, name="rise")
-        for k in (0, 1):
-            nc.vector.tensor_tensor(rise[:, part_cols(k)], neighbours(0, 2, PART * k, PART), lo0[:, part_cols(k)], SUB)
-
-        def finish_on_gpsimd(k):
-            step = keep.tile([P, PART], F32, name=f"step{k}", tag=f"step{k}")
-            nc.vector.scalar_tensor_tensor(step[:], rise[:, part_cols(k)], 0.0, spread[k][:], MAX, MIN)
-            med = keep.tile([P, PART], F32, name=f"med{k}")
-            nc.gpsimd.tensor_tensor(med[:], lo0[:, part_cols(k)], step[:], ADD)
-            store(k, med, nc.sync)
-
-        finish_on_gpsimd(0)
-        b1 = keep.tile([P, V], F32, name="b1", tag="turned0_1")
-        nc.vector.tensor_copy(b1[:], neighbours(1, 1, 0, V))
-        for k in (2, 3):
-            excess = close_difference(k, diff[k], b1[:, part_cols(k)], RELU)
-            for i, c in enumerate(squares):
-                transpose_add(upper[k][:, c], excess[i][:], False, i == per_part - 1)
-        finish_on_gpsimd(1)
-        c1 = keep.tile([P, V], F32, name="c1", tag="turned1_1")
-        nc.vector.tensor_copy(c1[:], neighbours(1, 2, 0, V))
-
-        lo1 = keep.tile([P, V], F32, name="lo1", tag="step1")
-        nc.vector.tensor_tensor(lo1[:], a1[:], b1[:], MIN)
-        below = keep.tile([P, V], F32, name="below")
-        for k in (2, 3):
-            nc.vector.tensor_tensor(below[:, part_cols(k)], c1[:, part_cols(k)], upper[k][:], MIN)
-        for k in (2, 3):
-            med = keep.tile([P, PART], F32, name=f"med{k}")
-            nc.vector.tensor_tensor(med[:], below[:, part_cols(k)], lo1[:, part_cols(k)], MAX)
-            store(k, med, nc.scalar)
+        got = [[keep.tile([P, V], F32, name=f"got{h}_{i}") for i in range(3)] for h in range(2)]
+        nc.vector.tensor_copy(got[0][0][:], neighbours(0, 0, 0, V))
+        nc.scalar.activation(got[0][1][:], neighbours(0, 1, 0, V), COPY)
+        nc.vector.tensor_copy(got[0][2][:], neighbours(0, 2, 0, V))
+        median(0, *got[0], nc.sync)
+        for i in range(2):
+            nc.scalar.activation(got[1][i][:], neighbours(1, i, 0, V), COPY)
+        for v in parts:
+            nc.scalar.activation(got[1][2][:, v], neighbours(1, 2, v.start, PART), COPY)
+        median(1, *got[1], nc.scalar)

@@ -88,37 +88,44 @@ def tile_picked_median_gelu_p_kernel(
             )
             return codes, plane
 
+        chunks = [(0, 512), (512, 256), (768, 256)]
         picked = [
-            placed.tile([P, CHUNK], U32, name="picked0", offset=2048, align_bytes=64),
-            placed.tile([P, CHUNK], U32, name="picked1", offset=4096, align_bytes=64),
+            placed.tile([P, 512], U32, name="picked0", offset=2048, align_bytes=64),
+            placed.tile([P, 256], U32, name="picked1", offset=4096, align_bytes=64),
+            placed.tile([P, 256], U32, name="picked2", offset=5120, align_bytes=64),
         ]
 
         def gather_words(c):
-            cols = slice(c * CHUNK // LANES, (c + 1) * CHUNK // LANES)
-            nc.vector.tensor_copy(picked[c][:], word_table[:].bitcast(U32).indirect(offs_t[:, cols]))
+            s0, n = chunks[c]
+            nc.vector.tensor_copy(picked[c][:], word_table[:].bitcast(U32).indirect(offs_t[:, s0 // LANES : (s0 + n) // LANES]))
 
         gather_words(0)
         nc.scalar.copy(*walks(0, 0, SPLIT))
         nc.gpsimd.tensor_scalar(*walks(0, SPLIT, P), 1.0, 0.0, MULT, ADD)
         w_q = [quantize_w(0)]
         gather_words(1)
+        gather_words(2)
         nc.vector.tensor_copy(*walks(1, 0, P))
         w_q.append(quantize_w(1))
 
-        pieces = [[(0, CHUNK)] + [(s0, P) for s0 in range(CHUNK, S, P)], [(0, CHUNK), (CHUNK, CHUNK)]]
+        pieces = [
+            [(0, 0, P), (0, P, P), (0, 256, 256), (1, 0, 256), (2, 0, P), (2, P, P)],
+            [(0, 0, 512), (1, 0, 256), (2, 0, 256)],
+        ]
         y = []
         bank = 0
         for h in range(2):
             codes, plane = w_q[h]
             y_h = keep.tile([P, S], F32, name=f"y{h}")
-            for s0, n in pieces[h]:
-                acc = psum.tile([P, n], F32, name=f"acc{h}_{s0}", tag=f"bank{bank}")
+            for c, j0, n in pieces[h]:
+                s0 = chunks[c][0] + j0
+                acc = psum.tile([P, n], F32, name=f"acc{h}_{s0}", tag=f"bank{bank % 8}")
                 bank = bank + 1
                 nc.tensor.matmul_mx(
                     out=acc[:],
                     lhsT=codes[:].bitcast(FP8X4),
                     lhsT_scale=plane[:],
-                    rhs=picked[s0 // CHUNK][:, s0 % CHUNK : s0 % CHUNK + n].bitcast(FP8X4),
+                    rhs=picked[c][:, j0 : j0 + n].bitcast(FP8X4),
                     rhs_scale=x_plane[:, s0 : s0 + n],
                     start=True,
                     stop=True,

@@ -44,17 +44,14 @@ def tile_picked_median_gelu_p_kernel(
         scale_table = placed.tile([P, T], U8, name="scale_table", offset=0, align_bytes=64)
         w_rows = w1.rearrange("(p j) m -> p j m", j=PACK)
         w_raw = [
-            placed.tile([P, PACK, P], F32, name="w_raw0", offset=4096, align_bytes=64),
+            placed.tile([P, PACK, P], F32, name="w_raw0", offset=5120, align_bytes=64),
             placed.tile([P, PACK, P], F32, name="w_raw1", offset=0, align_bytes=64),
         ]
         word_table = keep.tile([P, T], I32, name="word_table", align_bytes=64)
         nc.scalar.dma_start(scale_table[ROW0:P, :].bitcast(I32), x_scales[0].bitcast(I32))
         nc.sync.dma_start(offs_t[:], offs)
         nc.sync.dma_start(word_table[:], x_words[0].rearrange("p n t -> p (n t)").bitcast(I32))
-        nc.sync.dma_start(pos_t[0][:], pos1)
         nc.sync.dma_start(w_raw[0][:], w_rows[:, :, 0 * P : 1 * P])
-        nc.sync.dma_start(pos_t[1][:], pos2)
-        nc.sync.dma_start(pos_t[2][:], pos3)
         nc.vector.memset(scale_table[0:ROW0, :].bitcast(I32), 0)
 
         warm = keep.tile([P, 16], F32, name="warm")
@@ -71,6 +68,8 @@ def tile_picked_median_gelu_p_kernel(
                 picked_scales[ROW0 + 4 * q : ROW0 + 4 * q + 4, :].bitcast(I32),
             )
         nc.sync.dma_start(w_raw[1][:], w_rows[:, :, 1 * P : 2 * P])
+        for tile, pos in zip(pos_t, (pos1, pos2, pos3)):
+            nc.sync.dma_start(tile[:], pos)
 
         grouped = [keep.tile([P, P, PACK], BF16, name=f"w_grouped{h}", tag="w_grouped", align_bytes=64) for h in range(2)]
 
@@ -88,11 +87,10 @@ def tile_picked_median_gelu_p_kernel(
             )
             return codes, plane
 
-        chunks = [(0, 512), (512, 256), (768, 256)]
+        chunks = [(0, 768), (768, 256)]
         picked = [
-            placed.tile([P, 512], U32, name="picked0", offset=2048, align_bytes=64),
-            placed.tile([P, 256], U32, name="picked1", offset=4096, align_bytes=64),
-            placed.tile([P, 256], U32, name="picked2", offset=5120, align_bytes=64),
+            placed.tile([P, 768], U32, name="picked0", offset=2048, align_bytes=64),
+            placed.tile([P, 256], U32, name="picked1", offset=5120, align_bytes=64),
         ]
 
         def gather_words(c):
@@ -104,13 +102,12 @@ def tile_picked_median_gelu_p_kernel(
         nc.gpsimd.tensor_scalar(*walks(0, SPLIT, P), 1.0, 0.0, MULT, ADD)
         w_q = [quantize_w(0)]
         gather_words(1)
-        gather_words(2)
         nc.vector.tensor_copy(*walks(1, 0, P))
         w_q.append(quantize_w(1))
 
         pieces = [
-            [(0, 0, P), (0, P, P), (0, 256, 256), (1, 0, 256), (2, 0, P), (2, P, P)],
-            [(0, 0, 512), (1, 0, 256), (2, 0, 256)],
+            [(0, 0, P), (0, P, P), (0, 256, 256), (0, 512, 256), (1, 0, P), (1, P, P)],
+            [(0, 0, 512), (0, 512, 256), (1, 0, 256)],
         ]
         y = []
         bank = 0
@@ -133,31 +130,53 @@ def tile_picked_median_gelu_p_kernel(
                 nc.scalar.activation(y_h[:, s0 : s0 + n], acc[:], GELU)
             y.append(y_h)
 
-        def neighbours(h, i, v0, n):
-            return y[h][:].indirect(pos_t[i][:, v0 // LANES : (v0 + n) // LANES])
+        def neighbours(h, i, v):
+            return y[h][:].indirect(pos_t[i][:, v.start // LANES : v.stop // LANES])
 
-        parts = [slice(v0, v0 + PART) for v0 in range(0, V, PART)]
+        def results(name):
+            return [keep.tile([P, V], F32, name=f"{name}{h}") for h in range(2)]
 
-        def median(h, a, b, c, queue):
-            hi = keep.tile([P, V], F32, name=f"hi{h}")
-            lo = keep.tile([P, V], F32, name=f"lo{h}")
-            below = keep.tile([P, V], F32, name=f"below{h}")
-            med = keep.tile([P, V], F32, name=f"med{h}")
-            nc.vector.tensor_tensor(hi[:], a[:], b[:], MAX)
-            nc.vector.tensor_tensor(lo[:], a[:], b[:], MIN)
-            for v in parts:
-                nc.vector.tensor_tensor(below[:, v], c[:, v], hi[:, v], MIN)
-            for v in parts:
-                nc.vector.tensor_tensor(med[:, v], below[:, v], lo[:, v], MAX)
-                queue.dma_start(out[P * h : P * (h + 1), v], med[:, v])
+        a, b, c, hi, lo, below, med = (results(name) for name in ("a", "b", "c", "hi", "lo", "below", "med"))
+        whole = slice(0, V)
+        first, second = slice(0, PART), slice(PART, V)
 
-        got = [[keep.tile([P, V], F32, name=f"got{h}_{i}") for i in range(3)] for h in range(2)]
-        nc.vector.tensor_copy(got[0][0][:], neighbours(0, 0, 0, V))
-        nc.scalar.activation(got[0][1][:], neighbours(0, 1, 0, V), COPY)
-        nc.vector.tensor_copy(got[0][2][:], neighbours(0, 2, 0, V))
-        median(0, *got[0], nc.sync)
-        for i in range(2):
-            nc.scalar.activation(got[1][i][:], neighbours(1, i, 0, V), COPY)
-        for v in parts:
-            nc.scalar.activation(got[1][2][:, v], neighbours(1, 2, v.start, PART), COPY)
-        median(1, *got[1], nc.scalar)
+        def upper(h, v):
+            nc.vector.tensor_tensor(hi[h][:, v], a[h][:, v], b[h][:, v], MAX)
+
+        def lower(h, v):
+            nc.vector.tensor_tensor(lo[h][:, v], a[h][:, v], b[h][:, v], MIN)
+
+        def cap(h, v):
+            nc.vector.tensor_tensor(below[h][:, v], c[h][:, v], hi[h][:, v], MIN)
+
+        def finish(h, v):
+            nc.vector.tensor_tensor(med[h][:, v], below[h][:, v], lo[h][:, v], MAX)
+
+        def store(h, v, queue):
+            queue.dma_start(out[P * h : P * (h + 1), v], med[h][:, v])
+
+        def scalar_gather(dst, h, i, v):
+            nc.scalar.activation(dst[h][:, v], neighbours(h, i, v), COPY)
+
+        nc.vector.tensor_copy(a[0][:], neighbours(0, 0, whole))
+        scalar_gather(b, 0, 1, whole)
+        nc.vector.tensor_copy(c[0][:], neighbours(0, 2, whole))
+        upper(0, whole)
+        lower(0, whole)
+        for v in (first, second):
+            cap(0, v)
+        for v in (first, second):
+            finish(0, v)
+            store(0, v, nc.sync)
+        scalar_gather(a, 1, 0, whole)
+        for i, dst in ((1, b), (2, c)):
+            for v in (first, second):
+                scalar_gather(dst, 1, i, v)
+        upper(1, first)
+        lower(1, whole)
+        upper(1, second)
+        for v in (first, second):
+            cap(1, v)
+        for v in (first, second):
+            finish(1, v)
+            store(1, v, nc.scalar)

@@ -105,21 +105,17 @@ def tile_picked_median_gelu_p_kernel(
         nc.vector.tensor_copy(*walks(1, 0, P))
         w_q.append(quantize_w(1))
 
-        pieces = [
-            [(0, 0, P), (0, P, P), (0, 256, 256), (0, 512, 256), (1, 0, P), (1, P, P)],
-            [(0, 0, 512), (0, 512, 256), (1, 0, 256)],
-        ]
-        y = []
-        bank = 0
-        for h in range(2):
+        y = [keep.tile([P, S], F32, name=f"y{h}") for h in range(2)]
+
+        def product(h, bank, runs):
             codes, plane = w_q[h]
-            y_h = keep.tile([P, S], F32, name=f"y{h}")
-            for c, j0, n in pieces[h]:
+            start = chunks[runs[0][0]][0] + runs[0][1]
+            width = sum(n for c, j0, n in runs)
+            acc = psum.tile([P, width], F32, name=f"acc{h}_{start}", tag=f"bank{bank}")
+            for c, j0, n in runs:
                 s0 = chunks[c][0] + j0
-                acc = psum.tile([P, n], F32, name=f"acc{h}_{s0}", tag=f"bank{bank % 8}")
-                bank = bank + 1
                 nc.tensor.matmul_mx(
-                    out=acc[:],
+                    out=acc[:, s0 - start : s0 - start + n],
                     lhsT=codes[:].bitcast(FP8X4),
                     lhsT_scale=plane[:],
                     rhs=picked[c][:, j0 : j0 + n].bitcast(FP8X4),
@@ -127,8 +123,12 @@ def tile_picked_median_gelu_p_kernel(
                     start=True,
                     stop=True,
                 )
-                nc.scalar.activation(y_h[:, s0 : s0 + n], acc[:], GELU)
-            y.append(y_h)
+            nc.scalar.activation(y[h][:, start : start + width], acc[:], GELU)
+
+        for bank, run in enumerate([(0, 0, P), (0, P, P), (0, 256, 256), (0, 512, 256), (1, 0, P), (1, P, P)]):
+            product(0, bank, [run])
+        for bank, run in zip((6, 7, 0), [(0, 0, 256), (0, 256, 512), (1, 0, 256)]):
+            product(1, bank, [run])
 
         def neighbours(h, i, v):
             return y[h][:].indirect(pos_t[i][:, v.start // LANES : v.stop // LANES])
@@ -137,6 +137,7 @@ def tile_picked_median_gelu_p_kernel(
             return [keep.tile([P, V], F32, name=f"{name}{h}") for h in range(2)]
 
         a, b, c, hi, lo, below, med = (results(name) for name in ("a", "b", "c", "hi", "lo", "below", "med"))
+        b[0] = placed.tile([P, V], F32, name="b_first", offset=5120, align_bytes=64)
         whole = slice(0, V)
         first, second = slice(0, PART), slice(PART, V)
 
@@ -159,22 +160,23 @@ def tile_picked_median_gelu_p_kernel(
             nc.scalar.activation(dst[h][:, v], neighbours(h, i, v), COPY)
 
         nc.vector.tensor_copy(a[0][:], neighbours(0, 0, whole))
-        scalar_gather(b, 0, 1, whole)
         nc.vector.tensor_copy(c[0][:], neighbours(0, 2, whole))
-        upper(0, whole)
+        for v in (first, second):
+            scalar_gather(b, 0, 1, v)
+        upper(0, first)
         lower(0, whole)
+        upper(0, second)
         for v in (first, second):
             cap(0, v)
         for v in (first, second):
             finish(0, v)
             store(0, v, nc.sync)
         scalar_gather(a, 1, 0, whole)
-        for i, dst in ((1, b), (2, c)):
-            for v in (first, second):
-                scalar_gather(dst, 1, i, v)
-        upper(1, first)
+        scalar_gather(b, 1, 1, whole)
+        for v in (first, second):
+            scalar_gather(c, 1, 2, v)
+        upper(1, whole)
         lower(1, whole)
-        upper(1, second)
         for v in (first, second):
             cap(1, v)
         for v in (first, second):

@@ -127,7 +127,7 @@ def tile_picked_median_gelu_p_kernel(
 
         for bank, run in enumerate([(0, 0, P), (0, P, P), (0, 256, 256), (0, 512, 256), (1, 0, P), (1, P, P)]):
             product(0, bank, [run])
-        for bank, run in zip((6, 7, 0), [(0, 0, 256), (0, 256, 512), (1, 0, 256)]):
+        for bank, run in zip((6, 7, 0, 1), [(0, 0, 256), (0, 256, 256), (0, 512, 256), (1, 0, 256)]):
             product(1, bank, [run])
 
         def neighbours(h, i, v):

@@ -27,6 +27,7 @@ ROW0 = P - BLOCKS
 CHUNK = 512
 SPLIT = 64
 PART = 256
+OWN = 448
 
 
 def tile_picked_median_gelu_p_kernel(
@@ -160,12 +161,11 @@ def tile_picked_median_gelu_p_kernel(
             nc.scalar.activation(dst[h][:, v], neighbours(h, i, v), COPY)
 
         nc.vector.tensor_copy(a[0][:], neighbours(0, 0, whole))
+        nc.vector.tensor_copy(b[0][:, OWN:V], neighbours(0, 1, slice(OWN, V)))
         nc.vector.tensor_copy(c[0][:], neighbours(0, 2, whole))
-        for v in (first, second):
-            scalar_gather(b, 0, 1, v)
-        upper(0, first)
+        scalar_gather(b, 0, 1, slice(0, OWN))
+        upper(0, whole)
         lower(0, whole)
-        upper(0, second)
         for v in (first, second):
             cap(0, v)
         for v in (first, second):

@@ -24,10 +24,15 @@ PACK = 4
 LANES = 16
 BLOCKS = K // 32
 ROW0 = P - BLOCKS
-CHUNK = 512
+BANKS = 8
+FRONT = 768
+PIECE = 256
 SPLIT = 64
 PART = 256
-OWN = 448
+
+LOW = 0
+LOW_WORDS = LOW + PACK * P * 4
+HIGH = LOW_WORDS + FRONT * 4
 
 
 def tile_picked_median_gelu_p_kernel(
@@ -37,22 +42,21 @@ def tile_picked_median_gelu_p_kernel(
     with ExitStack() as ctx:
         keep = ctx.enter_context(tc.tile_pool(name="keep", bufs=1))
         psum = ctx.enter_context(tc.psum_pool(name="psum", bufs=1))
-
         placed = ctx.enter_context(tc.tile_pool(name="placed", bufs=1))
 
         offs_t = keep.tile([P, S // LANES], U16, name="offs_t")
         pos_t = [keep.tile([P, V // LANES], U16, name=f"pos_t{i}") for i in range(3)]
-        scale_table = placed.tile([P, T], U8, name="scale_table", offset=0, align_bytes=64)
+        scale_table = placed.tile([P, T], U8, name="scale_table", offset=LOW, align_bytes=64)
         w_rows = w1.rearrange("(p j) m -> p j m", j=PACK)
         w_raw = [
-            placed.tile([P, PACK, P], F32, name="w_raw0", offset=5120, align_bytes=64),
-            placed.tile([P, PACK, P], F32, name="w_raw1", offset=0, align_bytes=64),
+            placed.tile([P, PACK, P], F32, name="w_raw0", offset=HIGH, align_bytes=64),
+            placed.tile([P, PACK, P], F32, name="w_raw1", offset=LOW, align_bytes=64),
         ]
         word_table = keep.tile([P, T], I32, name="word_table", align_bytes=64)
         nc.scalar.dma_start(scale_table[ROW0:P, :].bitcast(I32), x_scales[0].bitcast(I32))
         nc.sync.dma_start(offs_t[:], offs)
         nc.sync.dma_start(word_table[:], x_words[0].rearrange("p n t -> p (n t)").bitcast(I32))
-        nc.sync.dma_start(w_raw[0][:], w_rows[:, :, 0 * P : 1 * P])
+        nc.sync.dma_start(w_raw[0][:], w_rows[:, :, 0:P])
         nc.vector.memset(scale_table[0:ROW0, :].bitcast(I32), 0)
 
         warm = keep.tile([P, 16], F32, name="warm")
@@ -68,79 +72,77 @@ def tile_picked_median_gelu_p_kernel(
                 x_plane[32 * q : 32 * q + 4, :].bitcast(I32),
                 picked_scales[ROW0 + 4 * q : ROW0 + 4 * q + 4, :].bitcast(I32),
             )
-        nc.sync.dma_start(w_raw[1][:], w_rows[:, :, 1 * P : 2 * P])
+        nc.sync.dma_start(w_raw[1][:], w_rows[:, :, P:N])
         for tile, pos in zip(pos_t, (pos1, pos2, pos3)):
             nc.sync.dma_start(tile[:], pos)
 
         grouped = [keep.tile([P, P, PACK], BF16, name=f"w_grouped{h}", tag="w_grouped", align_bytes=64) for h in range(2)]
 
-        def walks(h, c0, c1):
+        def walks(h, m0, m1):
             return (
-                grouped[h][:, c0:c1, :].rearrange("p (c i) j -> p c j i", i=4),
-                w_raw[h][:, :, c0:c1].rearrange("p j (c i) -> p c j i", i=4),
+                grouped[h][:, m0:m1, :].rearrange("p (g i) j -> p g j i", i=4),
+                w_raw[h][:, :, m0:m1].rearrange("p j (g i) -> p g j i", i=4),
             )
 
         def quantize_w(h):
             codes = keep.tile([P, P], U32, name=f"w_codes{h}", align_bytes=64)
             plane = keep.tile([P, P], U8, name=f"w_plane{h}", align_bytes=64)
             nc.vector.quantize_mx(
-                out=codes[:].bitcast(FP8X4), scales=plane[:], in_=grouped[h][:].rearrange("p c j -> p (c j)")
+                out=codes[:].bitcast(FP8X4), scales=plane[:], in_=grouped[h][:].rearrange("p m j -> p (m j)")
             )
             return codes, plane
 
-        chunks = [(0, 768), (768, 256)]
-        picked = [
-            placed.tile([P, 768], U32, name="picked0", offset=2048, align_bytes=64),
-            placed.tile([P, 256], U32, name="picked1", offset=5120, align_bytes=64),
-        ]
+        front = placed.tile([P, FRONT], U32, name="picked_front", offset=LOW_WORDS, align_bytes=64)
+        back = placed.tile([P, S - FRONT], U32, name="picked_back", offset=HIGH, align_bytes=64)
+        word_window = word_table[:].bitcast(U32)
 
-        def gather_words(c):
-            s0, n = chunks[c]
-            nc.vector.tensor_copy(picked[c][:], word_table[:].bitcast(U32).indirect(offs_t[:, s0 // LANES : (s0 + n) // LANES]))
-
-        gather_words(0)
+        nc.vector.tensor_copy(front[:], word_window.indirect(offs_t[:, 0 : FRONT // LANES]))
         nc.scalar.copy(*walks(0, 0, SPLIT))
         nc.gpsimd.tensor_scalar(*walks(0, SPLIT, P), 1.0, 0.0, MULT, ADD)
         w_q = [quantize_w(0)]
-        gather_words(1)
+        nc.vector.tensor_copy(back[:], word_window.indirect(offs_t[:, FRONT // LANES : S // LANES]))
         nc.vector.tensor_copy(*walks(1, 0, P))
         w_q.append(quantize_w(1))
 
         y = [keep.tile([P, S], F32, name=f"y{h}") for h in range(2)]
-
-        def product(h, bank, runs):
+        widths = [[P, P, PIECE, PIECE, PIECE], [PIECE] * (S // PIECE)]
+        bank = 0
+        for h in range(2):
             codes, plane = w_q[h]
-            start = chunks[runs[0][0]][0] + runs[0][1]
-            width = sum(n for c, j0, n in runs)
-            acc = psum.tile([P, width], F32, name=f"acc{h}_{start}", tag=f"bank{bank}")
-            for c, j0, n in runs:
-                s0 = chunks[c][0] + j0
+            s0 = 0
+            for n in widths[h]:
+                words = front[:, s0 : s0 + n] if s0 < FRONT else back[:, s0 - FRONT : s0 - FRONT + n]
+                acc = psum.tile([P, n], F32, name=f"acc{h}_{s0}", tag=f"bank{bank % BANKS}")
                 nc.tensor.matmul_mx(
-                    out=acc[:, s0 - start : s0 - start + n],
+                    out=acc[:],
                     lhsT=codes[:].bitcast(FP8X4),
                     lhsT_scale=plane[:],
-                    rhs=picked[c][:, j0 : j0 + n].bitcast(FP8X4),
+                    rhs=words.bitcast(FP8X4),
                     rhs_scale=x_plane[:, s0 : s0 + n],
                     start=True,
                     stop=True,
                 )
-            nc.scalar.activation(y[h][:, start : start + width], acc[:], GELU)
+                nc.scalar.activation(y[h][:, s0 : s0 + n], acc[:], GELU)
+                s0 = s0 + n
+                bank = bank + 1
 
-        for bank, run in enumerate([(0, 0, P), (0, P, P), (0, 256, 256), (0, 512, 256), (1, 0, P), (1, P, P)]):
-            product(0, bank, [run])
-        for bank, run in zip((6, 7, 0, 1), [(0, 0, 256), (0, 256, 256), (0, 512, 256), (1, 0, 256)]):
-            product(1, bank, [run])
+        def per_half(name):
+            return [keep.tile([P, V], F32, name=f"{name}{h}") for h in range(2)]
+
+        a, b = per_half("a"), per_half("b")
+        c = [placed.tile([P, V], F32, name="c0", offset=HIGH, align_bytes=64), keep.tile([P, V], F32, name="c1")]
+        hi, lo, below, med = (per_half(name) for name in ("hi", "lo", "below", "med"))
+        whole = slice(0, V)
+        parts = [slice(v0, v0 + PART) for v0 in range(0, V, PART)]
 
         def neighbours(h, i, v):
             return y[h][:].indirect(pos_t[i][:, v.start // LANES : v.stop // LANES])
 
-        def results(name):
-            return [keep.tile([P, V], F32, name=f"{name}{h}") for h in range(2)]
+        def vector_gather(dst, h, i, v):
+            nc.vector.tensor_copy(dst[h][:, v], neighbours(h, i, v))
 
-        a, b, c, hi, lo, below, med = (results(name) for name in ("a", "b", "c", "hi", "lo", "below", "med"))
-        b[0] = placed.tile([P, V], F32, name="b_first", offset=5120, align_bytes=64)
-        whole = slice(0, V)
-        first, second = slice(0, PART), slice(PART, V)
+        def scalar_gather(dst, h, i, v):
+            nc.scalar.activation(dst[h][:, v], neighbours(h, i, v), COPY)
 
         def upper(h, v):
             nc.vector.tensor_tensor(hi[h][:, v], a[h][:, v], b[h][:, v], MAX)
@@ -148,37 +150,26 @@ def tile_picked_median_gelu_p_kernel(
         def lower(h, v):
             nc.vector.tensor_tensor(lo[h][:, v], a[h][:, v], b[h][:, v], MIN)
 
-        def cap(h, v):
-            nc.vector.tensor_tensor(below[h][:, v], c[h][:, v], hi[h][:, v], MIN)
+        def finish(h, queue):
+            for v in parts:
+                nc.vector.tensor_tensor(below[h][:, v], c[h][:, v], hi[h][:, v], MIN)
+            for v in parts:
+                nc.vector.tensor_tensor(med[h][:, v], below[h][:, v], lo[h][:, v], MAX)
+                queue.dma_start(out[P * h : P * (h + 1), v], med[h][:, v])
 
-        def finish(h, v):
-            nc.vector.tensor_tensor(med[h][:, v], below[h][:, v], lo[h][:, v], MAX)
-
-        def store(h, v, queue):
-            queue.dma_start(out[P * h : P * (h + 1), v], med[h][:, v])
-
-        def scalar_gather(dst, h, i, v):
-            nc.scalar.activation(dst[h][:, v], neighbours(h, i, v), COPY)
-
-        nc.vector.tensor_copy(a[0][:], neighbours(0, 0, whole))
-        nc.vector.tensor_copy(b[0][:, OWN:V], neighbours(0, 1, slice(OWN, V)))
-        nc.vector.tensor_copy(c[0][:], neighbours(0, 2, whole))
-        scalar_gather(b, 0, 1, slice(0, OWN))
-        upper(0, whole)
+        vector_gather(a, 0, 0, whole)
+        for v in parts:
+            vector_gather(b, 0, 1, v)
+        scalar_gather(c, 0, 2, whole)
+        upper(0, parts[0])
         lower(0, whole)
-        for v in (first, second):
-            cap(0, v)
-        for v in (first, second):
-            finish(0, v)
-            store(0, v, nc.sync)
+        upper(0, parts[1])
+        finish(0, nc.sync)
+
         scalar_gather(a, 1, 0, whole)
         scalar_gather(b, 1, 1, whole)
-        for v in (first, second):
+        for v in parts:
             scalar_gather(c, 1, 2, v)
         upper(1, whole)
         lower(1, whole)
-        for v in (first, second):
-            cap(1, v)
-        for v in (first, second):
-            finish(1, v)
-            store(1, v, nc.scalar)
+        finish(1, nc.scalar)

@@ -25,7 +25,7 @@ LANES = 16
 BLOCKS = K // 32
 ROW0 = P - BLOCKS
 BANKS = 8
-FRONT = 768
+FRONT = 640
 PIECE = 256
 SPLIT = 64
 PART = 256
@@ -101,7 +101,7 @@ def tile_picked_median_gelu_p_kernel(
         nc.gpsimd.tensor_scalar(*walks(0, SPLIT, P), 1.0, 0.0, MULT, ADD)
         w_q = [quantize_w(0)]
         nc.vector.tensor_copy(back[:], word_window.indirect(offs_t[:, FRONT // LANES : S // LANES]))
-        nc.vector.tensor_copy(*walks(1, 0, P))
+        nc.gpsimd.tensor_scalar(*walks(1, 0, P), 1.0, 0.0, MULT, ADD)
         w_q.append(quantize_w(1))
 
         y = [keep.tile([P, S], F32, name=f"y{h}") for h in range(2)]
@@ -111,17 +111,19 @@ def tile_picked_median_gelu_p_kernel(
             codes, plane = w_q[h]
             s0 = 0
             for n in widths[h]:
-                words = front[:, s0 : s0 + n] if s0 < FRONT else back[:, s0 - FRONT : s0 - FRONT + n]
                 acc = psum.tile([P, n], F32, name=f"acc{h}_{s0}", tag=f"bank{bank % BANKS}")
-                nc.tensor.matmul_mx(
-                    out=acc[:],
-                    lhsT=codes[:].bitcast(FP8X4),
-                    lhsT_scale=plane[:],
-                    rhs=words.bitcast(FP8X4),
-                    rhs_scale=x_plane[:, s0 : s0 + n],
-                    start=True,
-                    stop=True,
-                )
+                cuts = [s0, FRONT, s0 + n] if s0 < FRONT < s0 + n else [s0, s0 + n]
+                for s1, s2 in zip(cuts, cuts[1:]):
+                    words = front[:, s1:s2] if s1 < FRONT else back[:, s1 - FRONT : s2 - FRONT]
+                    nc.tensor.matmul_mx(
+                        out=acc[:, s1 - s0 : s2 - s0],
+                        lhsT=codes[:].bitcast(FP8X4),
+                        lhsT_scale=plane[:],
+                        rhs=words.bitcast(FP8X4),
+                        rhs_scale=x_plane[:, s1:s2],
+                        start=True,
+                        stop=True,
+                    )
                 nc.scalar.activation(y[h][:, s0 : s0 + n], acc[:], GELU)
                 s0 = s0 + n
                 bank = bank + 1

@@ -105,7 +105,7 @@ def tile_picked_median_gelu_p_kernel(
         w_q.append(quantize_w(1))
 
         y = [keep.tile([P, S], F32, name=f"y{h}") for h in range(2)]
-        widths = [[P, P, PIECE, PIECE, PIECE], [PIECE] * (S // PIECE)]
+        widths = [[P, P, PIECE, P, P, P, P], [P, P, PIECE, PIECE, PIECE]]
         bank = 0
         for h in range(2):
             codes, plane = w_q[h]

@@ -30,9 +30,11 @@ PIECE = 256
 SPLIT = 64
 PART = 256
 
-LOW = 0
+Y0 = 0
+TABLE = Y0 + S * 4
+LOW = TABLE - 1024
 LOW_WORDS = LOW + PACK * P * 4
-HIGH = LOW_WORDS + FRONT * 4
+HIGH = TABLE + T
 
 
 def tile_picked_median_gelu_p_kernel(
@@ -46,7 +48,7 @@ def tile_picked_median_gelu_p_kernel(
 
         offs_t = keep.tile([P, S // LANES], U16, name="offs_t")
         pos_t = [keep.tile([P, V // LANES], U16, name=f"pos_t{i}") for i in range(3)]
-        scale_table = placed.tile([P, T], U8, name="scale_table", offset=LOW, align_bytes=64)
+        scale_table = placed.tile([P, T], U8, name="scale_table", offset=TABLE, align_bytes=64)
         w_rows = w1.rearrange("(p j) m -> p j m", j=PACK)
         w_raw = [
             placed.tile([P, PACK, P], F32, name="w_raw0", offset=HIGH, align_bytes=64),
@@ -76,7 +78,7 @@ def tile_picked_median_gelu_p_kernel(
         for tile, pos in zip(pos_t, (pos1, pos2, pos3)):
             nc.sync.dma_start(tile[:], pos)
 
-        grouped = [keep.tile([P, P, PACK], BF16, name=f"w_grouped{h}", tag="w_grouped", align_bytes=64) for h in range(2)]
+        grouped = [keep.tile([P, P, PACK], BF16, name=f"w_grouped{h}", align_bytes=64) for h in range(2)]
 
         def walks(h, m0, m1):
             return (
@@ -101,10 +103,10 @@ def tile_picked_median_gelu_p_kernel(
         nc.gpsimd.tensor_scalar(*walks(0, SPLIT, P), 1.0, 0.0, MULT, ADD)
         w_q = [quantize_w(0)]
         nc.vector.tensor_copy(back[:], word_window.indirect(offs_t[:, FRONT // LANES : S // LANES]))
-        nc.gpsimd.tensor_scalar(*walks(1, 0, P), 1.0, 0.0, MULT, ADD)
+        nc.scalar.copy(*walks(1, 0, P))
         w_q.append(quantize_w(1))
 
-        y = [keep.tile([P, S], F32, name=f"y{h}") for h in range(2)]
+        y = [placed.tile([P, S], F32, name="y0", offset=Y0, align_bytes=64), keep.tile([P, S], F32, name="y1")]
         widths = [[P, P, PIECE, P, P, P, P], [P, P, PIECE, PIECE, PIECE]]
         bank = 0
         for h in range(2):

@@ -25,16 +25,15 @@ LANES = 16
 BLOCKS = K // 32
 ROW0 = P - BLOCKS
 BANKS = 8
-FRONT = 640
+FRONT = 512
 PIECE = 256
 SPLIT = 64
 PART = 256
 
-Y0 = 0
-TABLE = Y0 + S * 4
-LOW = TABLE - 1024
+LOW = 0
 LOW_WORDS = LOW + PACK * P * 4
-HIGH = TABLE + T
+HIGH = LOW + T
+HIGH_WORDS = HIGH + 512
 
 
 def tile_picked_median_gelu_p_kernel(
@@ -48,17 +47,18 @@ def tile_picked_median_gelu_p_kernel(
 
         offs_t = keep.tile([P, S // LANES], U16, name="offs_t")
         pos_t = [keep.tile([P, V // LANES], U16, name=f"pos_t{i}") for i in range(3)]
-        scale_table = placed.tile([P, T], U8, name="scale_table", offset=TABLE, align_bytes=64)
+        scale_table = placed.tile([P, T], U8, name="scale_table", offset=LOW, align_bytes=64)
         w_rows = w1.rearrange("(p j) m -> p j m", j=PACK)
-        w_raw = [
-            placed.tile([P, PACK, P], F32, name="w_raw0", offset=HIGH, align_bytes=64),
-            placed.tile([P, PACK, P], F32, name="w_raw1", offset=LOW, align_bytes=64),
+        w_pairs = [
+            placed.tile([P, 2, P], F32, name=f"w_pair{u}", offset=HIGH + u * 2 * P * 4, align_bytes=64) for u in range(2)
         ]
+        w_raw1 = placed.tile([P, PACK, P], F32, name="w_raw1", offset=LOW, align_bytes=64)
         word_table = keep.tile([P, T], I32, name="word_table", align_bytes=64)
         nc.scalar.dma_start(scale_table[ROW0:P, :].bitcast(I32), x_scales[0].bitcast(I32))
         nc.sync.dma_start(offs_t[:], offs)
         nc.sync.dma_start(word_table[:], x_words[0].rearrange("p n t -> p (n t)").bitcast(I32))
-        nc.sync.dma_start(w_raw[0][:], w_rows[:, :, 0:P])
+        for u in range(2):
+            nc.sync.dma_start(w_pairs[u][:], w_rows[:, 2 * u : 2 * u + 2, 0:P])
         nc.vector.memset(scale_table[0:ROW0, :].bitcast(I32), 0)
 
         warm = keep.tile([P, 16], F32, name="warm")
@@ -74,17 +74,14 @@ def tile_picked_median_gelu_p_kernel(
                 x_plane[32 * q : 32 * q + 4, :].bitcast(I32),
                 picked_scales[ROW0 + 4 * q : ROW0 + 4 * q + 4, :].bitcast(I32),
             )
-        nc.sync.dma_start(w_raw[1][:], w_rows[:, :, P:N])
+        nc.sync.dma_start(w_raw1[:], w_rows[:, :, P:N])
         for tile, pos in zip(pos_t, (pos1, pos2, pos3)):
             nc.sync.dma_start(tile[:], pos)
 
-        grouped = [keep.tile([P, P, PACK], BF16, name=f"w_grouped{h}", align_bytes=64) for h in range(2)]
+        grouped = [keep.tile([P, P, PACK], BF16, name=f"w_grouped{h}", tag="w_grouped", align_bytes=64) for h in range(2)]
 
-        def walks(h, m0, m1):
-            return (
-                grouped[h][:, m0:m1, :].rearrange("p (g i) j -> p g j i", i=4),
-                w_raw[h][:, :, m0:m1].rearrange("p j (g i) -> p g j i", i=4),
-            )
+        def walks(rounded, raw):
+            return rounded.rearrange("p (g i) j -> p g j i", i=4), raw.rearrange("p j (g i) -> p g j i", i=4)
 
         def quantize_w(h):
             codes = keep.tile([P, P], U32, name=f"w_codes{h}", align_bytes=64)
@@ -95,37 +92,46 @@ def tile_picked_median_gelu_p_kernel(
             return codes, plane
 
         front = placed.tile([P, FRONT], U32, name="picked_front", offset=LOW_WORDS, align_bytes=64)
-        back = placed.tile([P, S - FRONT], U32, name="picked_back", offset=HIGH, align_bytes=64)
+        backs = [
+            placed.tile([P, PIECE], U32, name=f"picked_back{i}", offset=HIGH_WORDS + i * PIECE * 4, align_bytes=64)
+            for i in range(2)
+        ]
         word_window = word_table[:].bitcast(U32)
 
         nc.vector.tensor_copy(front[:], word_window.indirect(offs_t[:, 0 : FRONT // LANES]))
-        nc.scalar.copy(*walks(0, 0, SPLIT))
-        nc.gpsimd.tensor_scalar(*walks(0, SPLIT, P), 1.0, 0.0, MULT, ADD)
+        for u in range(2):
+            j = slice(2 * u, 2 * u + 2)
+            nc.scalar.copy(*walks(grouped[0][:, 0:SPLIT, j], w_pairs[u][:, :, 0:SPLIT]))
+            nc.gpsimd.tensor_scalar(*walks(grouped[0][:, SPLIT:P, j], w_pairs[u][:, :, SPLIT:P]), 1.0, 0.0, MULT, ADD)
         w_q = [quantize_w(0)]
-        nc.vector.tensor_copy(back[:], word_window.indirect(offs_t[:, FRONT // LANES : S // LANES]))
-        nc.scalar.copy(*walks(1, 0, P))
+        for i, back in enumerate(backs):
+            s0 = FRONT + i * PIECE
+            nc.vector.tensor_copy(back[:], word_window.indirect(offs_t[:, s0 // LANES : (s0 + PIECE) // LANES]))
+        nc.gpsimd.tensor_scalar(*walks(grouped[1][:], w_raw1[:]), 1.0, 0.0, MULT, ADD)
         w_q.append(quantize_w(1))
 
-        y = [placed.tile([P, S], F32, name="y0", offset=Y0, align_bytes=64), keep.tile([P, S], F32, name="y1")]
-        widths = [[P, P, PIECE, P, P, P, P], [P, P, PIECE, PIECE, PIECE]]
+        y = [keep.tile([P, S], F32, name=f"y{h}") for h in range(2)]
+        widths = [[P, P, PIECE, PIECE, P, P], [P, P, PIECE, PIECE, PIECE]]
         bank = 0
         for h in range(2):
             codes, plane = w_q[h]
             s0 = 0
             for n in widths[h]:
                 acc = psum.tile([P, n], F32, name=f"acc{h}_{s0}", tag=f"bank{bank % BANKS}")
-                cuts = [s0, FRONT, s0 + n] if s0 < FRONT < s0 + n else [s0, s0 + n]
-                for s1, s2 in zip(cuts, cuts[1:]):
-                    words = front[:, s1:s2] if s1 < FRONT else back[:, s1 - FRONT : s2 - FRONT]
-                    nc.tensor.matmul_mx(
-                        out=acc[:, s1 - s0 : s2 - s0],
-                        lhsT=codes[:].bitcast(FP8X4),
-                        lhsT_scale=plane[:],
-                        rhs=words.bitcast(FP8X4),
-                        rhs_scale=x_plane[:, s1:s2],
-                        start=True,
-                        stop=True,
-                    )
+                if s0 < FRONT:
+                    words = front[:, s0 : s0 + n]
+                else:
+                    i, s1 = divmod(s0 - FRONT, PIECE)
+                    words = backs[i][:, s1 : s1 + n]
+                nc.tensor.matmul_mx(
+                    out=acc[:],
+                    lhsT=codes[:].bitcast(FP8X4),
+                    lhsT_scale=plane[:],
+                    rhs=words.bitcast(FP8X4),
+                    rhs_scale=x_plane[:, s0 : s0 + n],
+                    start=True,
+                    stop=True,
+                )
                 nc.scalar.activation(y[h][:, s0 : s0 + n], acc[:], GELU)
                 s0 = s0 + n
                 bank = bank + 1
@@ -134,7 +140,7 @@ def tile_picked_median_gelu_p_kernel(
             return [keep.tile([P, V], F32, name=f"{name}{h}") for h in range(2)]
 
         a, b = per_half("a"), per_half("b")
-        c = [placed.tile([P, V], F32, name="c0", offset=HIGH, align_bytes=64), keep.tile([P, V], F32, name="c1")]
+        c = [placed.tile([P, V], F32, name="c0", offset=HIGH_WORDS, align_bytes=64), keep.tile([P, V], F32, name="c1")]
         hi, lo, below, med = (per_half(name) for name in ("hi", "lo", "below", "med"))
         whole = slice(0, V)
         parts = [slice(v0, v0 + PART) for v0 in range(0, V, PART)]
@@ -154,12 +160,11 @@ def tile_picked_median_gelu_p_kernel(
         def lower(h, v):
             nc.vector.tensor_tensor(lo[h][:, v], a[h][:, v], b[h][:, v], MIN)
 
-        def finish(h, queue):
+        def finish(h):
             for v in parts:
                 nc.vector.tensor_tensor(below[h][:, v], c[h][:, v], hi[h][:, v], MIN)
             for v in parts:
                 nc.vector.tensor_tensor(med[h][:, v], below[h][:, v], lo[h][:, v], MAX)
-                queue.dma_start(out[P * h : P * (h + 1), v], med[h][:, v])
 
         vector_gather(a, 0, 0, whole)
         for v in parts:
@@ -168,7 +173,8 @@ def tile_picked_median_gelu_p_kernel(
         upper(0, parts[0])
         lower(0, whole)
         upper(0, parts[1])
-        finish(0, nc.sync)
+        finish(0)
+        nc.sync.dma_start(out[0:P, :], med[0][:])
 
         scalar_gather(a, 1, 0, whole)
         scalar_gather(b, 1, 1, whole)
@@ -176,4 +182,6 @@ def tile_picked_median_gelu_p_kernel(
             scalar_gather(c, 1, 2, v)
         upper(1, whole)
         lower(1, whole)
-        finish(1, nc.scalar)
+        finish(1)
+        for v in parts:
+            nc.scalar.dma_start(out[P:N, v], med[1][:, v])

@@ -139,8 +139,8 @@ def tile_picked_median_gelu_p_kernel(
         def per_half(name):
             return [keep.tile([P, V], F32, name=f"{name}{h}") for h in range(2)]
 
-        a, b = per_half("a"), per_half("b")
-        c = [placed.tile([P, V], F32, name="c0", offset=HIGH_WORDS, align_bytes=64), keep.tile([P, V], F32, name="c1")]
+        a, c = per_half("a"), per_half("c")
+        b = [placed.tile([P, V], F32, name="b0", offset=HIGH_WORDS, align_bytes=64), keep.tile([P, V], F32, name="b1")]
         hi, lo, below, med = (per_half(name) for name in ("hi", "lo", "below", "med"))
         whole = slice(0, V)
         parts = [slice(v0, v0 + PART) for v0 in range(0, V, PART)]
@@ -154,34 +154,24 @@ def tile_picked_median_gelu_p_kernel(
         def scalar_gather(dst, h, i, v):
             nc.scalar.activation(dst[h][:, v], neighbours(h, i, v), COPY)
 
-        def upper(h, v):
-            nc.vector.tensor_tensor(hi[h][:, v], a[h][:, v], b[h][:, v], MAX)
-
-        def lower(h, v):
-            nc.vector.tensor_tensor(lo[h][:, v], a[h][:, v], b[h][:, v], MIN)
-
-        def finish(h):
+        def median(h):
+            nc.vector.tensor_tensor(hi[h][:], a[h][:], b[h][:], MAX)
+            nc.vector.tensor_tensor(lo[h][:], a[h][:], b[h][:], MIN)
             for v in parts:
                 nc.vector.tensor_tensor(below[h][:, v], c[h][:, v], hi[h][:, v], MIN)
             for v in parts:
                 nc.vector.tensor_tensor(med[h][:, v], below[h][:, v], lo[h][:, v], MAX)
 
         vector_gather(a, 0, 0, whole)
-        for v in parts:
-            vector_gather(b, 0, 1, v)
-        scalar_gather(c, 0, 2, whole)
-        upper(0, parts[0])
-        lower(0, whole)
-        upper(0, parts[1])
-        finish(0)
+        vector_gather(c, 0, 2, whole)
+        scalar_gather(b, 0, 1, whole)
+        median(0)
         nc.sync.dma_start(out[0:P, :], med[0][:])
 
         scalar_gather(a, 1, 0, whole)
         scalar_gather(b, 1, 1, whole)
         for v in parts:
             scalar_gather(c, 1, 2, v)
-        upper(1, whole)
-        lower(1, whole)
-        finish(1)
+        median(1)
         for v in parts:
             nc.scalar.dma_start(out[P:N, v], med[1][:, v])

@@ -28,10 +28,12 @@ BANKS = 8
 FRONT = 512
 PIECE = 256
 SPLIT = 64
+SPLIT_LATE = 80
 PART = 256
 
-LOW = 0
-LOW_WORDS = LOW + PACK * P * 4
+RAW = PACK * P * 4
+LOW = S * 4 - RAW
+LOW_WORDS = LOW + RAW
 HIGH = LOW + T
 HIGH_WORDS = HIGH + 512
 
@@ -107,11 +109,14 @@ def tile_picked_median_gelu_p_kernel(
         for i, back in enumerate(backs):
             s0 = FRONT + i * PIECE
             nc.vector.tensor_copy(back[:], word_window.indirect(offs_t[:, s0 // LANES : (s0 + PIECE) // LANES]))
-        nc.gpsimd.tensor_scalar(*walks(grouped[1][:], w_raw1[:]), 1.0, 0.0, MULT, ADD)
+        nc.scalar.copy(*walks(grouped[1][:, 0:SPLIT_LATE, :], w_raw1[:, :, 0:SPLIT_LATE]))
+        nc.gpsimd.tensor_scalar(
+            *walks(grouped[1][:, SPLIT_LATE:P, :], w_raw1[:, :, SPLIT_LATE:P]), 1.0, 0.0, MULT, ADD
+        )
         w_q.append(quantize_w(1))
 
-        y = [keep.tile([P, S], F32, name=f"y{h}") for h in range(2)]
-        widths = [[P, P, PIECE, PIECE, P, P], [P, P, PIECE, PIECE, PIECE]]
+        y = [placed.tile([P, S], F32, name="y0", offset=0), keep.tile([P, S], F32, name="y1")]
+        widths = [[PIECE, PIECE, PIECE, P, P], [P, P, PIECE, PIECE, PIECE]]
         bank = 0
         for h in range(2):
             codes, plane = w_q[h]

@@ -28,7 +28,7 @@ BANKS = 8
 FRONT = 512
 PIECE = 256
 SPLIT = 64
-SPLIT_LATE = 80
+SPLIT_LATE = 64
 PART = 256
 
 RAW = PACK * P * 4

@@ -28,12 +28,11 @@ BANKS = 8
 FRONT = 512
 PIECE = 256
 SPLIT = 64
-SPLIT_LATE = 64
 PART = 256
 
-RAW = PACK * P * 4
-LOW = S * 4 - RAW
-LOW_WORDS = LOW + RAW
+Y0 = 0
+LOW = Y0 + S * 4 - T // 2
+LOW_WORDS = Y0 + S * 4
 HIGH = LOW + T
 HIGH_WORDS = HIGH + 512
 
@@ -54,7 +53,9 @@ def tile_picked_median_gelu_p_kernel(
         w_pairs = [
             placed.tile([P, 2, P], F32, name=f"w_pair{u}", offset=HIGH + u * 2 * P * 4, align_bytes=64) for u in range(2)
         ]
-        w_raw1 = placed.tile([P, PACK, P], F32, name="w_raw1", offset=LOW, align_bytes=64)
+        y = [placed.tile([P, S], F32, name="y0", offset=Y0, align_bytes=64), keep.tile([P, S], F32, name="y1")]
+        raw0 = PIECE - SPLIT
+        w_raw1 = y[0][:, raw0 : raw0 + PACK * P].rearrange("p (j m) -> p j m", j=PACK)
         word_table = keep.tile([P, T], I32, name="word_table", align_bytes=64)
         nc.scalar.dma_start(scale_table[ROW0:P, :].bitcast(I32), x_scales[0].bitcast(I32))
         nc.sync.dma_start(offs_t[:], offs)
@@ -76,7 +77,7 @@ def tile_picked_median_gelu_p_kernel(
                 x_plane[32 * q : 32 * q + 4, :].bitcast(I32),
                 picked_scales[ROW0 + 4 * q : ROW0 + 4 * q + 4, :].bitcast(I32),
             )
-        nc.sync.dma_start(w_raw1[:], w_rows[:, :, P:N])
+        nc.sync.dma_start(w_raw1, w_rows[:, :, P:N])
         for tile, pos in zip(pos_t, (pos1, pos2, pos3)):
             nc.sync.dma_start(tile[:], pos)
 
@@ -109,13 +110,12 @@ def tile_picked_median_gelu_p_kernel(
         for i, back in enumerate(backs):
             s0 = FRONT + i * PIECE
             nc.vector.tensor_copy(back[:], word_window.indirect(offs_t[:, s0 // LANES : (s0 + PIECE) // LANES]))
-        nc.scalar.copy(*walks(grouped[1][:, 0:SPLIT_LATE, :], w_raw1[:, :, 0:SPLIT_LATE]))
+        nc.scalar.copy(*walks(grouped[1][:, 0:SPLIT, :], w_raw1[:, :, 0:SPLIT]))
         nc.gpsimd.tensor_scalar(
-            *walks(grouped[1][:, SPLIT_LATE:P, :], w_raw1[:, :, SPLIT_LATE:P]), 1.0, 0.0, MULT, ADD
+            *walks(grouped[1][:, SPLIT:P, :], w_raw1[:, :, SPLIT:P]), 1.0, 0.0, MULT, ADD
         )
         w_q.append(quantize_w(1))
 
-        y = [placed.tile([P, S], F32, name="y0", offset=0), keep.tile([P, S], F32, name="y1")]
         widths = [[PIECE, PIECE, PIECE, P, P], [P, P, PIECE, PIECE, PIECE]]
         bank = 0
         for h in range(2):

@@ -28,9 +28,12 @@ BANKS = 8
 FRONT = 512
 PIECE = 256
 SPLIT = 64
+RAW_STEP = 224
+SPLIT_LATE = 48
 PART = 256
 
 Y0 = 0
+RAW0 = PIECE - SPLIT_LATE - (S - PACK * RAW_STEP)
 LOW = Y0 + S * 4 - T // 2
 LOW_WORDS = Y0 + S * 4
 HIGH = LOW + T
@@ -54,8 +57,7 @@ def tile_picked_median_gelu_p_kernel(
             placed.tile([P, 2, P], F32, name=f"w_pair{u}", offset=HIGH + u * 2 * P * 4, align_bytes=64) for u in range(2)
         ]
         y = [placed.tile([P, S], F32, name="y0", offset=Y0, align_bytes=64), keep.tile([P, S], F32, name="y1")]
-        raw0 = PIECE - SPLIT
-        w_raw1 = y[0][:, raw0 : raw0 + PACK * P].rearrange("p (j m) -> p j m", j=PACK)
+        w_raw1 = y[0][:, S - PACK * RAW_STEP : S].rearrange("p (j m) -> p j m", j=PACK)[:, :, RAW0 : RAW0 + P]
         word_table = keep.tile([P, T], I32, name="word_table", align_bytes=64)
         nc.scalar.dma_start(scale_table[ROW0:P, :].bitcast(I32), x_scales[0].bitcast(I32))
         nc.sync.dma_start(offs_t[:], offs)
@@ -110,9 +112,9 @@ def tile_picked_median_gelu_p_kernel(
         for i, back in enumerate(backs):
             s0 = FRONT + i * PIECE
             nc.vector.tensor_copy(back[:], word_window.indirect(offs_t[:, s0 // LANES : (s0 + PIECE) // LANES]))
-        nc.scalar.copy(*walks(grouped[1][:, 0:SPLIT, :], w_raw1[:, :, 0:SPLIT]))
+        nc.scalar.copy(*walks(grouped[1][:, 0:SPLIT_LATE, :], w_raw1[:, :, 0:SPLIT_LATE]))
         nc.gpsimd.tensor_scalar(
-            *walks(grouped[1][:, SPLIT:P, :], w_raw1[:, :, SPLIT:P]), 1.0, 0.0, MULT, ADD
+            *walks(grouped[1][:, SPLIT_LATE:P, :], w_raw1[:, :, SPLIT_LATE:P]), 1.0, 0.0, MULT, ADD
         )
         w_q.append(quantize_w(1))
 

from contextlib import ExitStack

import concourse.mybir as mybir

K, T, S, V, N = 512, 4096, 1024, 512, 256
FLOPS = 2 * K * N * S

F32 = mybir.dt.float32
BF16 = mybir.dt.bfloat16
I32 = mybir.dt.int32
U32 = mybir.dt.uint32
U16 = mybir.dt.uint16
U8 = mybir.dt.uint8
FP8X4 = mybir.dt.float8_e4m3fn_x4
GELU = mybir.ActivationFunctionType.Gelu_apprx_tanh
COPY = mybir.ActivationFunctionType.Copy
MAX = mybir.AluOpType.max
MIN = mybir.AluOpType.min
ADD = mybir.AluOpType.add
MULT = mybir.AluOpType.mult

P = 128
PACK = 4
LANES = 16
BLOCKS = K // 32
ROW0 = P - BLOCKS
BANKS = 8
FRONT = 512
PIECE = 256
SPLIT = 64
RAW_STEP = 224
SPLIT_LATE = 48
PART = 256

Y0 = 0
RAW0 = PIECE - SPLIT_LATE - (S - PACK * RAW_STEP)
LOW = Y0 + S * 4 - T // 2
LOW_WORDS = Y0 + S * 4
HIGH = LOW + T
HIGH_WORDS = HIGH + 512


def tile_picked_median_gelu_p_kernel(
    tc, x_words, x_scales, w1, offs, pos1, pos2, pos3, out
):
    nc = tc.nc
    with ExitStack() as ctx:
        keep = ctx.enter_context(tc.tile_pool(name="keep", bufs=1))
        psum = ctx.enter_context(tc.psum_pool(name="psum", bufs=1))
        placed = ctx.enter_context(tc.tile_pool(name="placed", bufs=1))

        offs_t = keep.tile([P, S // LANES], U16, name="offs_t")
        pos_t = [keep.tile([P, V // LANES], U16, name=f"pos_t{i}") for i in range(3)]
        scale_table = placed.tile([P, T], U8, name="scale_table", offset=LOW, align_bytes=64)
        w_rows = w1.rearrange("(p j) m -> p j m", j=PACK)
        w_pairs = [
            placed.tile([P, 2, P], F32, name=f"w_pair{u}", offset=HIGH + u * 2 * P * 4, align_bytes=64) for u in range(2)
        ]
        y = [placed.tile([P, S], F32, name="y0", offset=Y0, align_bytes=64), keep.tile([P, S], F32, name="y1")]
        w_raw1 = y[0][:, S - PACK * RAW_STEP : S].rearrange("p (j m) -> p j m", j=PACK)[:, :, RAW0 : RAW0 + P]
        word_table = keep.tile([P, T], I32, name="word_table", align_bytes=64)
        nc.scalar.dma_start(scale_table[ROW0:P, :].bitcast(I32), x_scales[0].bitcast(I32))
        nc.sync.dma_start(offs_t[:], offs)
        nc.sync.dma_start(word_table[:], x_words[0].rearrange("p n t -> p (n t)").bitcast(I32))
        for u in range(2):
            nc.sync.dma_start(w_pairs[u][:], w_rows[:, 2 * u : 2 * u + 2, 0:P])
        nc.vector.memset(scale_table[0:ROW0, :].bitcast(I32), 0)

        warm = keep.tile([P, 16], F32, name="warm")
        nc.vector.memset(warm[:, 0:1], 0.0)
        nc.scalar.activation(warm[:, 8:9], warm[:, 0:1], GELU)

        picked_scales = keep.tile([P, S], U8, name="picked_scales", align_bytes=64)
        nc.vector.tensor_copy(picked_scales[:], scale_table[:].indirect(offs_t[:]))
        x_plane = keep.tile([P, S], U8, name="x_plane", align_bytes=64)
        nc.vector.memset(x_plane[:].bitcast(I32), 0)
        for q in range(4):
            nc.sync.dma_start(
                x_plane[32 * q : 32 * q + 4, :].bitcast(I32),
                picked_scales[ROW0 + 4 * q : ROW0 + 4 * q + 4, :].bitcast(I32),
            )
        nc.sync.dma_start(w_raw1, w_rows[:, :, P:N])
        for tile, pos in zip(pos_t, (pos1, pos2, pos3)):
            nc.sync.dma_start(tile[:], pos)

        grouped = [keep.tile([P, P, PACK], BF16, name=f"w_grouped{h}", tag="w_grouped", align_bytes=64) for h in range(2)]

        def walks(rounded, raw):
            return rounded.rearrange("p (g i) j -> p g j i", i=4), raw.rearrange("p j (g i) -> p g j i", i=4)

        def quantize_w(h):
            codes = keep.tile([P, P], U32, name=f"w_codes{h}", align_bytes=64)
            plane = keep.tile([P, P], U8, name=f"w_plane{h}", align_bytes=64)
            nc.vector.quantize_mx(
                out=codes[:].bitcast(FP8X4), scales=plane[:], in_=grouped[h][:].rearrange("p m j -> p (m j)")
            )
            return codes, plane

        front = placed.tile([P, FRONT], U32, name="picked_front", offset=LOW_WORDS, align_bytes=64)
        backs = [
            placed.tile([P, PIECE], U32, name=f"picked_back{i}", offset=HIGH_WORDS + i * PIECE * 4, align_bytes=64)
            for i in range(2)
        ]
        word_window = word_table[:].bitcast(U32)

        nc.vector.tensor_copy(front[:], word_window.indirect(offs_t[:, 0 : FRONT // LANES]))
        for u in range(2):
            j = slice(2 * u, 2 * u + 2)
            nc.scalar.copy(*walks(grouped[0][:, 0:SPLIT, j], w_pairs[u][:, :, 0:SPLIT]))
            nc.gpsimd.tensor_scalar(*walks(grouped[0][:, SPLIT:P, j], w_pairs[u][:, :, SPLIT:P]), 1.0, 0.0, MULT, ADD)
        w_q = [quantize_w(0)]
        for i, back in enumerate(backs):
            s0 = FRONT + i * PIECE
            nc.vector.tensor_copy(back[:], word_window.indirect(offs_t[:, s0 // LANES : (s0 + PIECE) // LANES]))
        nc.scalar.copy(*walks(grouped[1][:, 0:SPLIT_LATE, :], w_raw1[:, :, 0:SPLIT_LATE]))
        nc.gpsimd.tensor_scalar(
            *walks(grouped[1][:, SPLIT_LATE:P, :], w_raw1[:, :, SPLIT_LATE:P]), 1.0, 0.0, MULT, ADD
        )
        w_q.append(quantize_w(1))

        widths = [[PIECE, PIECE, PIECE, P, P], [P, P, PIECE, PIECE, PIECE]]
        bank = 0
        for h in range(2):
            codes, plane = w_q[h]
            s0 = 0
            for n in widths[h]:
                acc = psum.tile([P, n], F32, name=f"acc{h}_{s0}", tag=f"bank{bank % BANKS}")
                if s0 < FRONT:
                    words = front[:, s0 : s0 + n]
                else:
                    i, s1 = divmod(s0 - FRONT, PIECE)
                    words = backs[i][:, s1 : s1 + n]
                nc.tensor.matmul_mx(
                    out=acc[:],
                    lhsT=codes[:].bitcast(FP8X4),
                    lhsT_scale=plane[:],
                    rhs=words.bitcast(FP8X4),
                    rhs_scale=x_plane[:, s0 : s0 + n],
                    start=True,
                    stop=True,
                )
                nc.scalar.activation(y[h][:, s0 : s0 + n], acc[:], GELU)
                s0 = s0 + n
                bank = bank + 1

        def per_half(name):
            return [keep.tile([P, V], F32, name=f"{name}{h}") for h in range(2)]

        a, c = per_half("a"), per_half("c")
        b = [placed.tile([P, V], F32, name="b0", offset=HIGH_WORDS, align_bytes=64), keep.tile([P, V], F32, name="b1")]
        hi, lo, below, med = (per_half(name) for name in ("hi", "lo", "below", "med"))
        whole = slice(0, V)
        parts = [slice(v0, v0 + PART) for v0 in range(0, V, PART)]

        def neighbours(h, i, v):
            return y[h][:].indirect(pos_t[i][:, v.start // LANES : v.stop // LANES])

        def vector_gather(dst, h, i, v):
            nc.vector.tensor_copy(dst[h][:, v], neighbours(h, i, v))

        def scalar_gather(dst, h, i, v):
            nc.scalar.activation(dst[h][:, v], neighbours(h, i, v), COPY)

        def median(h):
            nc.vector.tensor_tensor(hi[h][:], a[h][:], b[h][:], MAX)
            nc.vector.tensor_tensor(lo[h][:], a[h][:], b[h][:], MIN)
            for v in parts:
                nc.vector.tensor_tensor(below[h][:, v], c[h][:, v], hi[h][:, v], MIN)
            for v in parts:
                nc.vector.tensor_tensor(med[h][:, v], below[h][:, v], lo[h][:, v], MAX)

        vector_gather(a, 0, 0, whole)
        vector_gather(c, 0, 2, whole)
        scalar_gather(b, 0, 1, whole)
        median(0)
        nc.sync.dma_start(out[0:P, :], med[0][:])

        scalar_gather(a, 1, 0, whole)
        scalar_gather(b, 1, 1, whole)
        for v in parts:
            scalar_gather(c, 1, 2, v)
        median(1)
        for v in parts:
            nc.scalar.dma_start(out[P:N, v], med[1][:, v])
